import numpy as np, ml_dtypes
CORES = [2,6,10,14,18,22,26,30]
N = 8
BF = ml_dtypes.bfloat16
def gentries(a):
    return np.ascontiguousarray(a.reshape(8, 16, -1).transpose(0, 2, 1)).reshape(8, -1)
def gtable(e):
    e = np.asarray(e); return np.ascontiguousarray(e.reshape(8, -1, 16).transpose(0, 2, 1)).reshape(128, -1).astype(np.int32)
def f(rng, *shape):
    return (rng.standard_normal(shape, dtype=np.float32) * np.exp2(rng.integers(-2, 3, shape[:-1] + (1,)))).astype(BF)
def wide(rng, *shape):
    v = f(rng, *shape).astype(np.float32); k = shape[:-2] + (1, shape[-1])
    return (v * np.exp2(rng.integers(-6, 7, k)) * (rng.random(k) > 0.0625)).astype(BF)
W, K, S, RO, FI, CAP = 6144, 1024, 3, 2, 8, 128
def parts(rng):
    b = rng.random((N, 8, S, W)) < rng.choice(np.array([0.5, 0.6, 0.75]), (N, 8, S, 1)); b[..., 0] = True; b[..., W - 1] = True
    nx = np.zeros((N, 8, S, W), np.int64); cur = np.zeros((N, 8, S, K), np.int64)
    for a in range(N):
        for g in range(8):
            for i in range(S):
                v = np.nonzero(b[a, g, i])[0]
                nx[a, g, i] = rng.choice(v, W); nx[a, g, i, v] = rng.permutation(v); cur[a, g, i] = rng.choice(v, K)
    return b, nx, cur, rng.integers(0, S, (N, 8, K)), rng.integers(0, W, (N, 8, W))
def pack(x, b, nx, cur, typ, fro, w):
    mem = np.add.reduce(b.astype(np.int64) << np.arange(S)[:, None], axis=2)
    return {"x": x.astype(BF).reshape(N, 128, W), "nxt": nx.reshape(N, 8, S * W).astype(np.int32), "mem": mem.astype(np.int32), "fro": fro.astype(np.int32),
            "cur": np.stack([gtable(a.reshape(8, S * K)) for a in cur]), "typ": np.stack([gtable(a) for a in typ]), "w0": w.astype(BF).reshape(N, 128, K)}
def setup_inputs(rng):
    b, nx, cur, typ, fro = parts(rng)
    return pack(f(rng, N, 128, W), b, nx, cur, typ, fro, f(rng, N, 128, K))
def setup_inputs_room(rng):
    b, nx, cur, typ, fro = parts(rng)
    x = np.minimum(f(rng, N, 128, W).astype(np.float32), 24); w = f(rng, N, 128, K).astype(np.float32).reshape(N, 8, 16, K)
    w[:, ::2] = np.abs(w[:, ::2]) + 32; w[:, 1] = np.abs(w[:, 1]) + 32
    at = np.take_along_axis(cur, typ[:, :, None, :], 2)[:, :, 0]
    for q in range(FI): at = np.take_along_axis(nx.reshape(N, 8, S * W), typ * W + at, 2)
    z = np.where(typ == S - 1, 0, typ + 1)
    for a in range(N):
        m, zz, cc, i = at[a, 1], z[a, 1], cur[a, 1], a % S
        o = rng.permutation(np.arange(1, K - 1)); o = o[b[a, 1, zz[o], m[o]] & (m[o] > 0) & (m[o] < W - 2)]
        o = rng.permutation(o[np.unique(m[o], return_index=True)[1]])
        by = [o[zz[o] == j] for j in range(S)]
        cc[zz, np.arange(K)] = m
        for j in range(S): cc[j, by[j][:3]] = (0, W - 2, W - 1)
        u, v, p, q, e1, e2 = by[i][3:9]
        ends = [K - 1, 0] if a % 2 == 0 else [0, K - 1]
        typ[a, 1, ends] = typ[a, 1, [u, v]]; cc[:, ends] = cc[:, [u, v]]
        cc[i, ends[0]] = m[q]; cc[i, p] = m[v]
        r = rng.choice(np.nonzero(~b[a, 1, i, :W - 2])[0]); nx[a, 1, i, r] = nx[a, 1, i, m[e1]]; cc[i, e1] = r; cc[i, e2] = r
        b[a, 1, typ[a, 1, [u, p]], m[[u, p]]] = False
    for a in range(N):
        for g in range(0, 8, 2):
            m = at[a, g]; zz = z[a, g]; e = rng.permutation(np.nonzero(b[a, g, zz, m])[0])
            k = int(rng.choice(np.array([0, 1, CAP - 1, CAP, CAP + 1, len(e)])))
            if a < 2: k = ((CAP, CAP + 1, CAP - 1, 0), (1, CAP, len(e), CAP + 1))[a][g // 2]
            cur[a, g, zz[e], e] = m[e]
            one = e[(zz[e] == 0) & (m[e] != 0)][:1] if k == 1 else e[:0]
            e = np.concatenate([one, e])[:k]; k = len(e)
            c = rng.choice(np.concatenate([rng.permutation(W)[:int(rng.choice(np.array([24, 150, 600, W])))], m[e[:k // 4]]]), k)
            cur[a, g, zz[e], e] = np.where(c == m[e], (c + 1) % W, c)
            cur[a, g, 0, one] = 0
    return pack(x, b, nx, cur, typ, fro, w)
def setup_inputs_ties(rng):
    b, nx, cur, typ, fro = parts(rng)
    x = 4.0 * rng.integers(-3, 4, (N, 8, 16, W)); w = 4.0 * rng.integers(-3, 4, (N, 8, 16, K))
    x[::2, 5] = rng.choice(np.array([7.96875, 8, 8, 8, 8.0625]), (N // 2, 16, W)); x[1::2, 5] = 64
    w[:, 5] = rng.choice(np.array([-1.0, 1.0]), (N, 16, K)) * np.exp2(-1.0 * rng.integers(14, 21, (N, 16, K)))
    return pack(x, b, nx, cur, typ, fro, w)
def setup_inputs_alike(rng):
    b, nx, cur, typ, fro = parts(rng)
    cur[:, 0] = rng.choice(np.array([0, W - 1]), (N, S, K)); nx[:, 1] = rng.choice(np.array([0, 3, W // 2, W - 1]), (N, S, W)); nx[:, 2] = np.arange(W)
    fro[:, 3] = rng.choice(np.array([0, W - 1]), (N, W)); b[:, 4] = True; b[:, 5] = False; typ[:, 6] = 0; cur[:, 7] = np.repeat(cur[:, 7, :1], S, axis=1)
    return pack(f(rng, N, 128, W), b, nx, cur, typ, fro, f(rng, N, 128, K))
def setup_inputs_hot(rng):
    b, nx, cur, typ, fro = parts(rng)
    sh = rng.choice(np.array([-64, 0, 64]), (N, 8, 1, 1)); sh[0, :4, 0, 0] = (-64, 64, -64, 0); sh[1, 4:, 0, 0] = (0, -64, 64, -64)
    b[rng.random((N, 8)) < 0.3] = True; b[0, 0] = True; b[1, 5] = True
    x = f(rng, N, 128, W).reshape(N, 8, 16, W); w = f(rng, N, 128, K).astype(np.float32).reshape(N, 8, 16, K) + sh
    for g in (3, 6):
        b[:, g] = True; w[:, g] = 4
        x[::2, g] = (rng.integers(0, 25, x[::2, g].shape) * 0.125).astype(BF); x[1::2, g] = (rng.integers(-32, -7, x[1::2, g].shape) * 0.125).astype(BF)
    for a in range(0, N, 2):
        o = np.concatenate([CAP // 2 + rng.permutation(CAP // 2)[:CAP // 4], CAP + rng.permutation(K - CAP)[:CAP // 8]])
        w[a, 6][:, o] = 1000
    return pack(x, b, nx, cur, typ, fro, w)
def setup_inputs_spread(rng):
    b, nx, cur, typ, fro = parts(rng)
    return pack(wide(rng, N, 128, W), b, nx, cur, typ, fro, wide(rng, N, 128, K))
def check_inputs(d):
    bad = []
    for k, hi in (("nxt", W - 1), ("mem", 2 ** S - 1), ("fro", W - 1), ("cur", W - 1), ("typ", S - 1)):
        if np.min(d[k]) < 0 or np.max(d[k]) > hi: bad.append("range of " + k)
    for k in ("x", "w0"):
        if not np.all(np.abs(d[k].astype(np.float32)) < 2.0 ** 60): bad.append("size of " + k)
    return bad
def reference(x, nxt, mem, fro, cur, typ, w0):
    pick = np.take_along_axis
    X = x.astype(np.float32).reshape(N, 8, 16, W); w = w0.astype(np.float32).reshape(N, 8, 16, K)
    nx = nxt.astype(np.int64); mb = mem.astype(np.int64); fo = fro.astype(np.int64)
    c = np.stack([gentries(a) for a in cur]).astype(np.int64).reshape(N, 8, S, K); s = np.stack([gentries(a) for a in typ]).astype(np.int64)
    for t in range(RO):
        for q in range(FI):
            at = pick(c, s[:, :, None, :], 2)[:, :, 0]
            m = pick(nx, s * W + at, 2)
            hit = np.add.reduce((pick(X, m[:, :, None, :], 3) >= w).astype(np.int64), axis=2) >= 9
            bits = pick(mb, m, 2)
            for i in range(S): c[:, :, i] = np.where((s == i) | (hit & (((bits >> i) & 1) == 1)), m, c[:, :, i])
            s = np.where(hit, np.where(s == S - 1, 0, s + 1), s)
        z = np.where(s == S - 1, 0, s + 1)
        m = pick(c, s[:, :, None, :], 2)[:, :, 0]; e = pick(c, z[:, :, None, :], 2)[:, :, 0]
        want = (((pick(mb, m, 2) >> z) & 1) == 1) & (m != e)
        slot = want & (np.add.accumulate(want.astype(np.int64), axis=2) <= CAP)
        for a in range(N):
            for g in range(8):
                j = np.nonzero(slot[a, g])[0]
                p1 = z[a, g, j] * W + m[a, g, j]; p2 = z[a, g, j] * W + e[a, g, j]
                named = np.bincount(np.concatenate([p1, p2]), minlength=S * W)
                ok = (named[p1] == 1) & (named[p2] == 1); p1 = p1[ok]; p2 = p2[ok]
                v1 = nx[a, g, p1]; v2 = nx[a, g, p2]
                nx[a, g, p1] = v2; nx[a, g, p2] = v1
        k = pick(fo, m, 2)
        y = np.stack([pick(X[(a + 1 + t) % N], k[a][:, None, :], 2) for a in range(N)])
        w = w + np.minimum(np.maximum(y - w, np.float32(-8)), np.float32(8))
    return {"yc": np.stack([gtable(a.reshape(8, S * K)) for a in c]).astype(np.float32), "yw": w.reshape(N, 128, K).astype(np.float32), "yn": nx.astype(np.float32)}

@@ -1,0 +1,577 @@
+from concourse.mybir import AluOpType, ActivationFunctionType
+
+A = AluOpType
+AF = ActivationFunctionType
+W, K, NT, ROUNDS, FINDS, CAP = 6144, 1024, 3, 2, 8, 128
+H = K // 2
+STAMP = 8192
+BIG = 1 << 17
+NEQ = 4
+MS = 3
+FB, CB, PB, LB = 0.05, 0.3, 0.8, 0.15
+SB, BF, FP, I32, U16 = "sbuf", "bfloat16", "float32", "int32", "uint16"
+SCRATCH = {
+    "xs": (SB, [128, W], BF), "x1": (SB, [128, W], BF), "x2": (SB, [128, W], BF),
+    "inf": (SB, [128, W], BF), "pw": (SB, [128, 3 * W + 2 * CAP], BF),
+    "wb": (SB, [128, K], BF), "wf": (SB, [128, K], FP), "dd": (SB, [128, K], FP),
+    "n32": (SB, [128, 1152], I32), "nhi": (SB, [128, 1152], BF), "nlo": (SB, [128, 1152], BF),
+    "m32": (SB, [128, 384], I32), "mi": (SB, [128, 768], I32), "bits": (SB, [128, 1152], BF),
+    "f32": (SB, [128, 384], I32), "fhi": (SB, [128, 384], BF), "flo": (SB, [128, 384], BF),
+    "pv": (SB, [128, 1152], FP), "phi": (SB, [128, 1152], BF), "plo": (SB, [128, 1152], BF),
+    "cur32": (SB, [128, 192], I32), "typ32": (SB, [128, 64], I32), "tf": (SB, [128, 64], FP),
+    "lst": (SB, [128, 192], U16), "ci": (SB, [128, 192], I32), "cj": (SB, [128, 192], I32), "ycf": (SB, [128, 192], FP),
+    "ones": (SB, [128, 192], BF), "idf": (SB, [128, 8, 4, 4], FP), "idb": (SB, [128, 128], BF), "idn": (SB, [128, 8 * 128], BF),
+    "stl": (SB, [128, 128 * (FINDS + 1)], BF), "c72": (SB, [128, 128], BF),
+    "wnx": (SB, [128, 24], BF), "wv": (SB, [128, 24], BF), "wx": (SB, [128, 48], BF), "wbit": (SB, [128, 24], BF), "wcnt": (SB, [128, 48], BF),
+    "sel": (SB, [128, 32], FP), "selr": (SB, [128, 32], FP),
+    "pid": (SB, [128, 1], I32), "pm": (SB, [128, 4], I32), "cols": (SB, [128, 16], FP),
+    "bo": (SB, [128, 128], BF), "lm": (SB, [128, 128], BF), "plw": (SB, [128, 128], BF),
+    "eqm": (SB, [128, 16, 8, 16], BF), "dm": (SB, [128, 16, 8, 16], BF), "dp": (SB, [128, 16, 8, 16], BF),
+    "db": (SB, [128, 16, 8, 16], BF), "df": (SB, [128, 16, 8, 16], BF),
+    "kc": (SB, [128, 8], FP), "kch": (SB, [128, 8], FP), "dumc": (SB, [128, 16], FP), "kio": (SB, [128, 128], FP),
+    "ttl": (SB, [128, 256], FP), "eq": (SB, [128, 256 * NEQ], BF),
+    "mz": (SB, [128, 128], FP), "mzi": (SB, [128, 128], I32), "mzj": (SB, [128, 128], I32), "mp4": (SB, [128, 32, 4], FP),
+    "lte": (SB, [128, 32, 4, 4], FP), "ltc": (SB, [128, 48, 4, 4], FP),
+    "ot": (SB, [128, 128], U16), "otf": (SB, [128, 64], FP), "nq": (SB, [128, 64], BF),
+    "ra": (SB, [128, K + 16], BF), "rb": (SB, [128, K + 16], BF),
+    "wt": (SB, [128, 64], BF), "pc": (SB, [128, 64], BF), "rt": (SB, [128, 72], FP), "junk": (SB, [128, 512], BF),
+    "ck": (SB, [128, 8], FP), "ckl": (SB, [128, 8], U16), "ckb": (SB, [128, 8], BF), "le": (SB, [128, 128], BF), "jk": (SB, [128, 8], U16),
+    "sab": (SB, [128, 256], BF), "plr": (SB, [128, 256], U16), "plt": (SB, [128, 16], FP),
+    "cb": (SB, [128, 128], BF), "cp": (SB, [128, 128], FP), "dab": (SB, [128, 128], FP), "dmv": (SB, [128, 128], FP),
+    "nv": (SB, [128, 256], BF), "pd": (SB, [128, 16], FP), "of": (SB, [128, 16], FP), "og": (SB, [128, 16], FP), "ofl": (SB, [128, 16], U16),
+    "kl": (SB, [128, 64], U16), "yh": (SB, [128, 1152], BF), "yl": (SB, [128, 1152], BF), "yf": (SB, [128, 1152], FP),
+}
+for _b in range(2):
+    for _n, _s, _d in (("ge", [128, H], BF), ("rw", [128, H], BF), ("off", [128, 32], U16), ("st", [128, 192], FP), ("gt", [128, 192], BF),
+                       ("sg", [128, 192], BF), ("ab", [128, 96], FP), ("tt", [128, 96], FP), ("tu", [128, 32], FP), ("mp", [128, 8, 4], FP),
+                       ("lt", [128, 8, 4, 4], FP), ("oi", [128, 32], I32), ("oj", [128, 32], I32)):
+        SCRATCH["%s%d" % (_n, _b)] = (SB, _s, _d)
+for _i in range(8):
+    SCRATCH["b%d" % _i] = ("psum", [128, 512], FP)
+ENG = {"V": "cv", "S": "cs", "P": "cp_", "G": "cg"}
+DMAS = ["l_m", "l_c", "l_t", "l_x", "l_w", "l_f", "d_i0", "d_i1", "d_i2", "d_bi", "d_fl", "d_pf", "d_pw", "d_rb", "d_y1", "d_yc", "d_yw0", "d_yw1", "d_yn1"]
+SEMAPHORES = sorted(ENG.values()) + DMAS + ["rx1", "rx2", "tx"]
+
+
+def rank_program(g, core, T, topo):
+    rank = T.rank_of(core)
+    if rank is None:
+        return
+    N = len(T.cores)
+    queues = {"V": g.vector, "S": g.scalar, "P": g.tensor, "G": g, "Y": g.sync}
+    clock = {q: {} for q in queues}
+    total = {}
+    snap = {}
+    acc = {}
+    free = {q: 0.0 for q in queues}
+    done = {}
+    rec = [None]
+
+    def know(q, sem, val):
+        c = clock[q]
+        if c.get(sem, 0) >= val:
+            return
+        queues[q].wait_ge(T.sem[sem], val)
+        for s, v in snap.get((sem, val), {}).items():
+            if v > c.get(s, 0):
+                c[s] = v
+        c[sem] = val
+
+    def region(r):
+        buf, lo, hi, tag = (r + (0, 1 << 20, None))[:4] if len(r) == 1 else (r + (None,))[:4]
+        if SCRATCH.get(buf, ("", 0, 0))[0] == "psum":
+            return buf, 0, 512, None, True
+        return buf, lo, hi, tag, False
+
+    def needs(q, reads, writes, dma):
+        need = {}
+        t = free[q]
+        for lst, wr in ((reads, False), (writes, True)):
+            for r in lst:
+                buf, lo, hi, tag, bank = region(r)
+                for a in acc.get(buf, ()):
+                    if a[1] <= lo or hi <= a[0] or (tag is not None and a[2] is not None and a[2] != tag):
+                        continue
+                    same = a[3] == q and not dma and a[4] not in DMAS
+                    if not (wr or a[6]) and (not bank or same):
+                        continue
+                    if same and (q == "P" or not a[6]):
+                        continue
+                    need[a[4]] = max(need.get(a[4], 0), a[5])
+                    t = max(t, done.get((a[4], a[5]), 0.0) + 0.06)
+        return need, t
+
+    def emit(q, fn, reads, writes, dma, cost):
+        need, t = needs(q, reads, writes, dma)
+        for s in sorted(need):
+            know(q, s, total[s] if s in DMAS else need[s])
+        ins = fn(queues[q])
+        sem, inc = (dma, 16) if dma else (ENG[q], 1)
+        ins.then_inc(T.sem[sem], inc)
+        total[sem] = total.get(sem, 0) + inc
+        val = total[sem]
+        s = dict(clock[q])
+        for k2, v2 in snap.get((sem, val - inc), {}).items():
+            s[k2] = max(v2, s.get(k2, 0))
+        s[sem] = val
+        snap[(sem, val)] = s
+        free[q] = t + (0.06 if dma else cost)
+        done[(sem, val)] = t + (4.0 if dma else cost)
+        for lst, wr in ((writes, True), (reads, False)):
+            for r in lst:
+                buf, lo, hi, tag, bank = region(r)
+                keep = []
+                for a in acc.get(buf, []):
+                    inside = lo <= a[0] and a[1] <= hi and (tag is None or tag == a[2])
+                    if inside and (wr or (not a[6] and a[3] == q and a[4] == sem)):
+                        continue
+                    keep.append(a)
+                keep.append((lo, hi, tag, q, sem, val, wr))
+                acc[buf] = keep
+
+    def op(q, fn, reads, writes, dma=None, cost=0.1):
+        if rec[0] is not None:
+            rec[0].append((q, fn, reads, writes, dma, cost))
+        else:
+            emit(q, fn, reads, writes, dma, cost)
+
+    def record(f, *args):
+        rec[0] = []
+        f(*args)
+        r, rec[0] = rec[0], None
+        return r
+
+    def merge(*streams):
+        st = [[s, 0, b] for s, b in streams]
+        while True:
+            best = None
+            for x in st:
+                if x[1] < len(x[0]):
+                    o = x[0][x[1]]
+                    t = needs(o[0], o[2], o[3], o[4])[1] + x[2]
+                    if best is None or t < best[0]:
+                        best = (t, x)
+            if best is None:
+                return
+            x = best[1]
+            emit(*x[0][x[1]])
+            x[1] += 1
+
+    scaled = [(T.idn[:, 128 * n:128 * n + 128], ("idn", 128 * n, 128 * n + 128)) for n in range(8)]
+    I16, IH, IMH, IM, IBIG, IW1, IW2, IPEN = scaled
+
+    def cols(ap):
+        n = 1
+        for d in list(ap.shape)[1:]:
+            n *= d
+        return n
+
+    def us(cycles):
+        return 0.03 + 0.00104 * cycles
+
+    def tt(q, out, o, a, ra, b, rb, f):
+        n = cols(out)
+        bank = any(region(r)[4] for r in (ra, rb))
+        op(q, lambda e: e.tensor_tensor(out, a, b, f), [ra, rb], [o], None, us(max(64, n if bank else 2 * n)))
+
+    def ts(out, o, a, ra, s1, s2, f1, f2=None, extra=()):
+        c = us(max(64, cols(out)))
+        if f2 is None:
+            op("V", lambda e: e.tensor_scalar(out, a, s1, None, f1), [ra] + list(extra), [o], None, c)
+        else:
+            op("V", lambda e: e.tensor_scalar(out, a, s1, s2, f1, f2), [ra] + list(extra), [o], None, c)
+
+    def cpy(out, o, a, ra):
+        op("V", lambda e: e.tensor_copy(out, a), [ra], [o], None, us(max(64, cols(out))))
+
+    def act(out, o, a, ra, f, bias=0.0, scale=1.0, extra=(), accum=None, ao=None):
+        c = us(cols(out))
+        if accum is None:
+            op("S", lambda e: e.activation(out, a, f, bias=bias, scale=scale), [ra] + list(extra), [o], None, c)
+        else:
+            op("S", lambda e: e.activation(out, a, f, bias=bias, scale=scale, accum_out=accum), [ra] + list(extra), [o, ao], None, c)
+
+    def mm(out, bank, l, rl, r, rr, start, stop):
+        op("P", lambda e: e.matmul(out, l, r, start, stop), [rl, rr], [(bank,)], None, max(64, cols(r)) * (0.0024 if rl[0][:2] in ("lt", "tt") else 0.0006))
+
+    def dma(q, out, o, a, ra, sem):
+        op(q, lambda e: e.dma_start(out, a), [ra] if ra else [], [o] if o else [], dma=sem)
+
+    def fill(name, v, lo=None, hi=None):
+        if lo is None:
+            op("V", lambda e: e.memset(T[name][:], v), [], [(name,)])
+        else:
+            op("V", lambda e: e.memset(T[name][:, lo:hi], v), [], [(name, lo, hi)])
+
+    def aff(out, src, pat, cmp, base, mult):
+        op("G", lambda e: e.affine_select(T[out][:], T[src][:], pat, cmp, 0.0, base, mult), [(src,)], [(out,)])
+
+    def gather(q, out, oreg, win, wn, n0, n1, off, offreg):
+        src = win[:, n0:n1].indirect(off)
+        c = us(1.5 * cols(out))
+        if q == "V":
+            op("V", lambda e: e.tensor_copy(out, src), [(wn, n0, n1), offreg], [oreg], None, c)
+        else:
+            op("S", lambda e: e.activation(out, src, AF.Copy), [(wn, n0, n1), offreg], [oreg], None, c)
+
+    for i in range(NT):
+        dma("Y", T.n32[:, 384 * i:384 * i + 384], ("n32", 384 * i, 384 * i + 384), T.nxt[:, W * i:W * i + W], None, "d_i%d" % i)
+    dma("S", T.m32[:], ("m32",), T.mem[:], None, "l_m")
+    dma("S", T.cur32[:], ("cur32",), T.cur[:], None, "l_c")
+    dma("S", T.typ32[:], ("typ32",), T.typ[:], None, "l_t")
+    dma("S", T.wb[:], ("wb",), T.w0[:], None, "l_w")
+    for k in range(11, 16):
+        dma("Y", T.inf[k::16, :], ("inf", 0, W, k), T.x[k::16, :], None, "d_fl")
+
+    fill("ones", 1.0)
+    for n in ("wnx", "wv", "wcnt"):
+        fill(n, 1.0)
+    fill("wbit", 16.0)
+    fill("idf", 1.0)
+    fill("sel", 1.0)
+    for t in range(FINDS + 1):
+        fill("stl", float(BIG // 128) if t == 0 else float(STAMP // 128 * t), 128 * t, 128 * t + 128)
+    for be in range(2):
+        fill("gt%d" % be, 0.0, 96, 192)
+    fill("bo", 1.0)
+    fill("eqm", 1.0)
+    op("G", lambda e: e.iota(T.pid[:], [[1, 1]], 0, 1), [], [("pid",)])
+    op("G", lambda e: e.iota(T.pv[:], [[W, 3], [1, 384]], 0, 384, allow_small_or_imprecise_dtypes=True), [], [("pv",)])
+    aff("idf", "idf", [[-1, 128]], A.is_equal, 0, 1)
+    aff("sel", "sel", [[-4, 32]], A.is_ge, 0, 1)
+    aff("sel", "sel", [[4, 32]], A.is_ge, 3, -1)
+    aff("wnx", "wnx", [[-2, 3], [-16, 8]], A.is_ge, 0, 1)
+    aff("wnx", "wnx", [[2, 3], [16, 8]], A.is_ge, 1, -1)
+    aff("wv", "wv", [[0, 3], [-16, 8]], A.is_ge, -9, 1)
+    aff("wv", "wv", [[0, 3], [16, 8]], A.is_ge, 10, -1)
+    aff("wcnt", "wcnt", [[0, 6], [-16, 8]], A.is_ge, 0, 1)
+    aff("wcnt", "wcnt", [[0, 6], [16, 8]], A.is_ge, 15, -1)
+    aff("wbit", "wbit", [[-1, 3], [-16, 8]], A.is_equal, -6, 1)
+    pm, co = T.pm, T.cols
+    ts(pm[:, 0:1], ("pm", 0, 1), T.pid[:], ("pid",), 3, None, A.bitwise_and)
+    ts(pm[:, 1:2], ("pm", 1, 2), T.pid[:], ("pid",), 2, 3, A.arith_shift_right, A.bitwise_and)
+    ts(pm[:, 2:3], ("pm", 2, 3), T.pid[:], ("pid",), 15, None, A.bitwise_and)
+    ts(pm[:, 3:4], ("pm", 3, 4), T.pid[:], ("pid",), 4, None, A.arith_shift_right)
+    for h in range(4):
+        ts(co[:, h:h + 1], ("cols", h, h + 1), pm[:, 0:1], ("pm", 0, 1), h, None, A.is_equal)
+        ts(co[:, 4 + h:5 + h], ("cols", 4 + h, 5 + h), pm[:, 1:2], ("pm", 1, 2), h, None, A.is_equal)
+    ts(co[:, 9:10], ("cols", 9, 10), pm[:, 3:4], ("pm", 3, 4), -W, None, A.mult)
+    ts(co[:, 10:11], ("cols", 10, 11), pm[:, 2:3], ("pm", 2, 3), 2, None, A.is_lt)
+    ts(co[:, 11:12], ("cols", 11, 12), pm[:, 3:4], ("pm", 3, 4), -16, None, A.mult)
+
+    def split(hi, lo, src, n0, n1, scalar=False):
+        if scalar:
+            act(T[hi][:, n0:n1], (hi, n0, n1), T[src][:, n0:n1], (src, n0, n1), AF.Copy)
+        else:
+            cpy(T[hi][:, n0:n1], (hi, n0, n1), T[src][:, n0:n1], (src, n0, n1))
+        tt("V", T[lo][:, n0:n1], (lo, n0, n1), T[src][:, n0:n1], (src, n0, n1), T[hi][:, n0:n1], (hi, n0, n1), A.subtract)
+
+    def to_inf(k, src, n0):
+        dma("Y", T.inf[k::16, :], ("inf", 0, W, k), T[src][:, n0:n0 + 384], (src, n0, n0 + 384), "d_bi")
+
+    def to_pw(k, i, src, n0):
+        dma("Y", T.pw[k::16, W * i:W * i + W], ("pw", W * i, W * i + W, k), T[src][:, n0:n0 + 384], (src, n0, n0 + 384), "d_pw")
+
+    act(T.pv[:], ("pv",), T.pv[:], ("pv",), AF.Identity, bias=co[:, 9:10], extra=[("cols", 9, 10)])
+    split("phi", "plo", "pv", 0, 384, True)
+    to_inf(9, "phi", 0)
+    to_inf(10, "plo", 0)
+    for i in range(NT):
+        split("nhi", "nlo", "n32", 384 * i, 384 * i + 384)
+        to_inf(2 * i, "nhi", 384 * i)
+        to_inf(2 * i + 1, "nlo", 384 * i)
+    ts(T.mi[:, 0:384], ("mi", 0, 384), T.m32[:], ("m32",), 1, None, A.bitwise_and)
+    ts(T.mi[:, 384:768], ("mi", 384, 768), T.m32[:], ("m32",), 2, None, A.bitwise_and)
+    ts(T.bits[:, 768:1152], ("bits", 768, 1152), T.m32[:], ("m32",), 4, None, A.is_ge)
+    ts(T.bits[:, 0:768], ("bits", 0, 768), T.mi[:], ("mi",), 1, None, A.is_ge)
+    for i in range(NT):
+        to_inf(6 + i, "bits", 384 * i)
+    dma("Y", T.xs[:], ("xs",), T.x[:], None, "l_x")
+    act(T.wf[:], ("wf",), T.wb[:], ("wb",), AF.Copy)
+    dma("S", T.f32[:], ("f32",), T.fro[:], None, "l_f")
+
+    cpy(T.lst[:], ("lst",), T.cur32[:], ("cur32",))
+    cpy(T.tf[:], ("tf",), T.typ32[:], ("typ32",))
+    cpy(T.idb[:], ("idb",), T.idf[:], ("idf",))
+    for n, v in enumerate((16.0, 0.5, -0.5, -1.0, float(BIG), W / 2.0, float(W), float(4 * BIG))):
+        ts(T.idn[:, 128 * n:128 * n + 128], ("idn", 128 * n, 128 * n + 128), T.idb[:], ("idb",), v, None, A.mult)
+    tt("V", T.selr[:], ("selr",), T.idf[:, :, 0, :], ("idf",), T.idf[:, :, 1, :], ("idf",), A.add)
+    for h in (2, 3):
+        tt("V", T.selr[:], ("selr",), T.selr[:], ("selr",), T.idf[:, :, h, :], ("idf",), A.add)
+    cpy(T.wx[:, 0:24], ("wx", 0, 24), T.wnx[:], ("wnx",))
+    cpy(T.wx[:, 24:48], ("wx", 24, 48), T.wv[:], ("wv",))
+
+    aff("bo", "bo", [[-16, 8], [0, 16]], A.is_ge, 0, 1)
+    aff("bo", "bo", [[16, 8], [0, 16]], A.is_ge, 15, -1)
+    aff("plw", "bo", [[-16, 8], [0, 16]], A.is_ge, -2, 1)
+    aff("plw", "plw", [[16, 8], [0, 16]], A.is_ge, 3, -1)
+    aff("lm", "bo", [[-1, 128]], A.is_gt, 0, 1)
+    op("G", lambda e: e.iota(T.kc[:], [[16, 8]], 0, 1, allow_small_or_imprecise_dtypes=True), [], [("kc",)])
+    op("G", lambda e: e.iota(T.kio[:], [[1, 128]], 0, 0, allow_small_or_imprecise_dtypes=True), [], [("kio",)])
+
+    know("G", "l_x", total["l_x"])
+    total["tx"] = 0
+    for t, buf in ((0, "x1"), (1, "x2")):
+        dst, src = T.cores[(rank - 1 - t) % N], T.cores[(rank + 1 + t) % N]
+        rid, pid, _s = topo.addr(dst)
+        rx = "rx%d" % (t + 1)
+        g.remote_dma(T[buf][:], T.xs[:], T.sem[rx], T.sem.tx, pid, rid, topo.mask(core, dst))
+        total["tx"] += len(topo.engines(core, dst))
+        total[rx] = len(topo.engines(src, core))
+        acc[buf] = [(0, 1 << 20, None, "R", rx, total[rx], True)]
+
+    aff("eqm", "eqm", [[1, 16], [0, 8], [-1, 16]], A.is_equal, 0, 0)
+    aff("db", "eqm", [[0, 16], [-16, 8], [0, 16]], A.is_equal, -4, 1)
+    aff("df", "eqm", [[0, 16], [-16, 8], [0, 16]], A.is_ge, -5, 1)
+    aff("df", "df", [[0, 16], [16, 8], [0, 16]], A.is_ge, 6, -1)
+    aff("dm", "eqm", [[0, 16], [-16, 8], [0, 16]], A.is_ge, 0, 1)
+    aff("dm", "dm", [[0, 16], [16, 8], [0, 16]], A.is_ge, 15, -1)
+    aff("dp", "eqm", [[0, 16], [-16, 8], [0, 16]], A.is_ge, -2, 1)
+    aff("dp", "dp", [[0, 16], [16, 8], [0, 16]], A.is_ge, 3, -1)
+
+    def later():
+        for i in range(1, NT):
+            split("phi", "plo", "pv", 384 * i, 384 * i + 384, True)
+        split("fhi", "flo", "f32", 0, 384)
+        for i in range(NT):
+            for k, (src, n0) in enumerate((("nhi", 384 * i), ("nlo", 384 * i), ("phi", 384 * i), ("plo", 384 * i), ("bits", 384 * i), ("fhi", 0), ("flo", 0))):
+                to_pw(k, i, src, n0)
+        for i in range(NT):
+            for k in range(7, 16):
+                dma("Y", T.pw[k::16, W * i:W * i + W], ("pw", W * i, W * i + W, k), T.x[k::16, :], None, "d_pf")
+        ts(T.kc[:], ("kc",), T.kc[:], ("kc",), co[:, 11:12], None, A.add, extra=[("cols", 11, 12)])
+        ts(T.kch[:], ("kch",), T.kc[:], ("kc",), 0.5, None, A.add)
+        ts(T.dumc[:, 0:8], ("dumc", 0, 8), T.kc[:], ("kc",), 3 * W, None, A.add)
+        ts(T.dumc[:, 8:16], ("dumc", 8, 16), T.kc[:], ("kc",), 3 * W + CAP, None, A.add)
+        ts(T.lm[:], ("lm",), T.lm[:], ("lm",), -1.0, None, A.mult)
+        fill("c72", 1.5 * W / 128)
+        fill("rt", 65536.0, 64, 72)
+        fill("ra", 16384.0, K, K + 16)
+        fill("rb", 16384.0, K, K + 16)
+
+    def masks(out, obuf, n0, n1, src, sreg, nscalar):
+        for h in range(4):
+            o = (obuf, n0, n1, h)
+            if h < nscalar:
+                act(out(h), o, src, sreg, AF.Copy, scale=co[:, h:h + 1], extra=[("cols", h, h + 1)])
+            else:
+                ts(out(h), o, src, sreg, co[:, h:h + 1], None, A.mult, extra=[("cols", h, h + 1)])
+
+    def types_in():
+        for be in range(2):
+            for h in range(4):
+                ts(T.ttl[:, 128 * be + h:128 * be + 128:4], ("ttl", 128 * be, 128 * be + 128, h), T.tf[:, 32 * be:32 * be + 32], ("tf",), co[:, 4 + h:5 + h], None, A.mult, extra=[("cols", 4 + h, 5 + h)])
+            O, ob = T["b%d" % (6 + be)], "b%d" % (6 + be)
+            mm(O[:, 0:32], ob, T.ttl[:, 128 * be:128 * be + 128], ("ttl", 128 * be, 128 * be + 128), T.selr[:], ("selr",), True, True)
+            ab, gt = "ab%d" % be, "gt%d" % be
+            for i in range(NT):
+                act(T[ab][:, 32 * i:32 * i + 32], (ab, 32 * i, 32 * i + 32), O[:, 0:32], (ob,), AF.Abs, bias=-float(i))
+            act(T[gt][:, 0:96], (gt, 0, 96), T[ab][:], (ab,), AF.Sign, bias=0.5, scale=-1.0)
+
+    def pick(be, s0):
+        st, gt, t, u = T["st%d" % be], T["gt%d" % be], T["tt%d" % be], T["tu%d" % be]
+        P, pb = T["b%d" % (4 + be)], "b%d" % (4 + be)
+        mm(P[:, 128:224], pb, *IPEN, gt[:, 0:96], ("gt%d" % be, 0, 96), True, True)
+        tt("V", t[:], ("tt%d" % be,), P[:, 128:224], (pb,), st[:, s0:s0 + 96], ("st%d" % be, s0, s0 + 96), A.add)
+        tt("V", u[:], ("tu%d" % be,), t[:, 0:32], ("tt%d" % be,), t[:, 32:64], ("tt%d" % be,), A.max)
+
+    def next_list(be, more=None):
+        t, u, mp, lt = T["tt%d" % be], T["tu%d" % be], T["mp%d" % be], T["lt%d" % be]
+        pick(be, 0)
+        tt("V", mp[:], ("mp%d" % be,), u[:], ("tu%d" % be,), t[:, 64:96], ("tt%d" % be,), A.max)
+        masks(lambda h: lt[:, :, h, :], "lt%d" % be, 0, 128, mp[:], ("mp%d" % be,), MS)
+        if more:
+            more()
+        O, ob = T["b%d" % (6 + be)], "b%d" % (6 + be)
+        mm(O[:, 0:32], ob, lt[:], ("lt%d" % be,), T.sel[:], ("sel",), True, True)
+        oi, oj, off = "oi%d" % be, "oj%d" % be, "off%d" % be
+        cpy(T[oi][:], (oi,), O[:, 0:32], (ob,))
+        ts(T[oj][:], (oj,), T[oi][:], (oi,), STAMP - 1, None, A.bitwise_and)
+        cpy(T[off][:], (off,), T[oj][:], (oj,))
+
+    def round_start(be):
+        X, xb, st = T["b%d" % be], "b%d" % be, "st%d" % be
+        mm(X[:, 0:192], xb, T.stl[:, 0:128], ("stl",), T.ones[:], ("ones",), True, False)
+        for i in range(NT):
+            buf = ("rw%d" if i % 2 == 0 else "ge%d") % be
+            l0 = 64 * i + 32 * be
+            gather("S" if (i + be) % 2 == 0 else "V", T[buf][:], (buf,), T.inf, "inf", 0, W, T.lst[:, l0:l0 + 32], ("lst",))
+            for b in range(4):
+                mm(X[:, 32 * i + b:32 * i + 32:4], xb, T[buf][:, b::4], (buf,), T.wx[:, 8 * i:8 * i + 8], ("wx",), False, False)
+                mm(X[:, 96 + 32 * i + b:128 + 32 * i:4], xb, T[buf][:, b::4], (buf,), T.wx[:, 24 + 8 * i:32 + 8 * i], ("wx",), False, i == NT - 1 and b == 3)
+        cpy(T[st][:], (st,), X[:, 0:192], (xb,))
+        next_list(be)
+
+    def find(be, q, last):
+        ge, rw, off, gt = "ge%d" % be, "rw%d" % be, "off%d" % be, "gt%d" % be
+        sg, ab, st = "sg%d" % be, "ab%d" % be, "st%d" % be
+        (X, xb), (Y, yb), (Z, zb) = [(T["b%d" % (n + be)], "b%d" % (n + be)) for n in (0, 2, 4)]
+        src = T.xs[:, 0:W].indirect(T[off][:])
+        op("V", lambda e: e.tensor_tensor(T[ge][:], src, T.wf[:, H * be:H * be + H], A.is_ge), [("xs",), (off,), ("wf", H * be, H * be + H)], [(ge,)], None, us(1.5 * H))
+        gather("S", T[rw][:], (rw,), T.inf, "inf", 0, W, T[off][:], (off,))
+        mm(Y[:, 0:192], yb, *I16, T[gt][:], (gt,), True, False)
+        mm(X[:, 0:192], xb, T.stl[:, 128 * (q + 1):128 * (q + 2)], ("stl",), T.ones[:], ("ones",), True, False)
+        mm(Z[:, 0:96], zb, *IH, T[gt][:, 0:96], (gt, 0, 96), True, False)
+        mm(Z[:, 0:32], zb, *IMH, T[gt][:, 64:96], (gt, 0, 96), False, False)
+        mm(Z[:, 32:96], zb, *IMH, T[gt][:, 0:64], (gt, 0, 96), False, False)
+        for b in range(4):
+            mm(Y[:, b:96:4], yb, T[rw][:, b::4], (rw,), T.wbit[:], ("wbit",), False, False)
+        for b in range(4):
+            mm(Y[:, b:192:4], yb, T[ge][:, b::4], (ge,), T.wcnt[:], ("wcnt",), False, b == 3)
+        for b in range(4):
+            mm(X[:, b:192:4], xb, T[rw][:, b::4], (rw,), T.wx[:], ("wx",), False, False)
+        act(T[sg][:], (sg,), Y[:, 0:192], (yb,), AF.Sign, bias=-8.5)
+        mm(Z[:, 0:96], zb, *IM, T[sg][:, 96:192], (sg,), False, True)
+        mm(X[:, 0:96], xb, *IBIG, T[sg][:, 0:96], (sg,), False, False)
+        mm(X[:, 96:192], xb, *IBIG, T[sg][:, 0:96], (sg,), False, True)
+        act(T[ab][:], (ab,), Z[:, 0:96], (zb,), AF.Abs)
+        act(T[gt][:, 0:96], (gt, 0, 96), T[ab][:], (ab,), AF.Sign, bias=-1.5)
+        tt("V", T[st][:, 0:96], (st, 0, 96), X[:, 0:96], (xb,), T[st][:, 0:96], (st, 0, 96), A.max)
+
+        def cursors_too():
+            tt("V", T[st][:, 96:192], (st, 96, 192), X[:, 96:192], (xb,), T[st][:, 96:192], (st, 96, 192), A.max)
+        if last:
+            cursors_too()
+        else:
+            next_list(be, cursors_too)
+
+    def finds(be):
+        round_start(be)
+        for q in range(FINDS):
+            find(be, q, q == FINDS - 1)
+
+    def diag(bank, c0, c1, d, src, s0, s1, start=True, stop=True):
+        for i in range(16):
+            mm(T[bank][:, c0:c1], bank, T[d][:, i, :, :], (d,), T[src][:, s0 + i:s1:16], (src, s0, s1), start and i == 0, stop and i == 15)
+
+    def places():
+        for be in range(2):
+            st, gt, tb, ub, ab, mp = [n % be for n in ("st%d", "gt%d", "tt%d", "tu%d", "ab%d", "mp%d")]
+            pick(be, 96)
+            tt("V", T.mz[:, 32 * be:32 * be + 32], ("mz", 32 * be, 32 * be + 32), T[ub][:], (ub,), T[tb][:, 64:96], (tb,), A.max)
+            tt("V", T[ab][:, 0:32], (ab, 0, 32), T[st][:, 96:128], (st,), T[gt][:, 64:96], (gt, 0, 96), A.mult)
+            tt("V", T[ab][:, 32:96], (ab, 32, 96), T[st][:, 128:192], (st,), T[gt][:, 0:64], (gt, 0, 96), A.mult)
+            tt("V", T[mp][:], (mp,), T[ab][:, 0:32], (ab,), T[ab][:, 32:64], (ab,), A.max)
+            tt("V", T.mz[:, 64 + 32 * be:96 + 32 * be], ("mz", 64 + 32 * be, 96 + 32 * be), T[mp][:], (mp,), T[ab][:, 64:96], (ab,), A.max)
+        mm(T.b6[:, 0:128], "b6", T.c72[:], ("c72",), T.ones[:, 0:128], ("ones",), True, False)
+        for s in range(2):
+            for be in range(2):
+                o = T.b6[:, 64 * s + 32 * be:64 * s + 32 * be + 32]
+                gt = "gt%d" % be
+                mm(o, "b6", *IW1, T[gt][:, 0:32], (gt, 0, 96), False, False)
+                mm(o, "b6", *IW2, T[gt][:, 32:64], (gt, 0, 96), False, s == 1 and be == 1)
+        cpy(T.mzi[:], ("mzi",), T.mz[:], ("mz",))
+        ts(T.mzj[:], ("mzj",), T.mzi[:], ("mzi",), STAMP - 1, None, A.bitwise_and)
+        tt("V", T.mp4[:], ("mp4",), T.b6[:, 0:128], ("b6",), T.mzj[:], ("mzj",), A.add)
+        masks(lambda h: T.lte[:, :, h, :], "lte", 0, 512, T.mp4[:], ("mp4",), 2)
+        for n in range(4):
+            mm(T.b7[:, 32 * n:32 * n + 32], "b7", T.lte[:, 8 * n:8 * n + 8, :, :], ("lte",), T.sel[:], ("sel",), True, True)
+        cpy(T.ot[:], ("ot",), T.b7[:, 0:128], ("b7",))
+        gather("V", T.ra[:, 0:H], ("ra", 0, H), T.pw, "pw", 0, 3 * W, T.ot[:, 0:32], ("ot",))
+        gather("S", T.ra[:, H:K], ("ra", H, K), T.pw, "pw", 0, 3 * W, T.ot[:, 32:64], ("ot",))
+        gather("S", T.rb[:, 256:K], ("rb", 256, K), T.pw, "pw", 0, 3 * W, T.ot[:, 80:128], ("ot",))
+        gather("V", T.rb[:, 0:256], ("rb", 0, 256), T.pw, "pw", 0, 3 * W, T.ot[:, 64:80], ("ot",))
+        cpy(T.otf[:], ("otf",), T.b7[:, 0:64], ("b7",))
+        tt("V", T.nq[:], ("nq",), T.b7[:, 64:128], ("b7",), T.otf[:], ("otf",), A.not_equal)
+
+    def swap(last):
+        diag("b2", 0, 64, "db", "ra", 0, K)
+        tt("V", T.wt[:], ("wt",), T.b2[:, 0:64], ("b2",), T.nq[:], ("nq",), A.mult)
+        op("V", lambda e: e.tensor_tensor_scan(T.pc[:], T.ones[:, 0:64], T.wt[:], 0.0, A.mult, A.add), [("ones",), ("wt",)], [("pc",)])
+        mm(T.b3[:, 0:64], "b3", T.bo[:], ("bo",), T.pc[:], ("pc",), True, True)
+        mm(T.b2[:, 64:128], "b2", T.bo[:], ("bo",), T.pc[:], ("pc",), True, False)
+        mm(T.b2[:, 64:128], "b2", T.lm[:], ("lm",), T.wt[:], ("wt",), False, True)
+        cpy(T.rt[:, 0:64], ("rt", 0, 64), T.b2[:, 64:128], ("b2",))
+        for n in range(8):
+            act(T.junk[:, 64 * n:64 * n + 64], ("junk", 64 * n, 64 * n + 64), T.b3[:, 0:64], ("b3",), AF.Sign, bias=T.kch[:, n:n + 1], scale=-1.0, extra=[("kch",)], accum=T.ck[:, n:n + 1], ao=("ck", n, n + 1))
+        ts(T.ckl[:], ("ckl",), T.ck[:], ("ck",), 0.5, 32.0, A.mult, A.add)
+        src = T.rt[:, 0:72].indirect(T.ckl[:])
+        op("V", lambda e: e.tensor_tensor(T.le[:], src, T.kio[:], A.is_le), [("rt",), ("ckl",), ("kio",)], [("le",)])
+        ts(T.ckb[:], ("ckb",), T.ck[:], ("ck",), 0.5, 32.0, A.mult, A.add)
+        diag("b2", 0, 8, "dm", "le", 0, 128, True, False)
+        mm(T.b2[:, 0:8], "b2", *I16, T.ckb[:], ("ckb",), False, True)
+        cpy(T.jk[:], ("jk",), T.b2[:, 0:8], ("b2",))
+        gather("V", T.sab[:, 0:128], ("sab", 0, 128), T.ra, "ra", 0, K + 16, T.jk[:], ("jk",))
+        gather("S", T.sab[:, 128:256], ("sab", 128, 256), T.rb, "rb", 0, K + 16, T.jk[:], ("jk",))
+        mm(T.b3[:, 0:256], "b3", T.plw[:], ("plw",), T.sab[:], ("sab",), True, True)
+        diag("b6", 0, 16, "dp", "sab", 0, 256)
+        cpy(T.plr[:], ("plr",), T.b3[:, 0:256], ("b3",))
+        cpy(T.plt[:], ("plt",), T.b6[:, 0:16], ("b6",))
+        for n in range(16):
+            a = 256 * (n % NEQ)
+            ts(T.eq[:, a:a + 256], ("eq", a, a + 256), T.plr[:], ("plr",), T.plt[:, n:n + 1], None, A.is_equal, extra=[("plt",)])
+            for s in range(2):
+                mm(T.b7[:, 0:128], "b7", T.bo[:], ("bo",), T.eq[:, a + 128 * s:a + 128 * s + 128], ("eq", a, a + 256), n == 0 and s == 0, n == 15 and s == 1)
+        tt("V", T.dab[:], ("dab",), T.sab[:, 128:256], ("sab",), T.sab[:, 0:128], ("sab",), A.subtract)
+        tt("V", T.pd[:], ("pd",), T.plt[:], ("plt",), T.dumc[:], ("dumc",), A.subtract)
+        ts(T.cb[:], ("cb",), T.b7[:, 0:128], ("b7",), 2.0, 1.0 / 16, A.is_equal, A.mult)
+        ts(T.cp[:], ("cp",), T.b7[:, 0:128], ("b7",), 2.0, co[:, 10:11], A.is_equal, A.mult, extra=[("cols", 10, 11)])
+        diag("b3", 0, 8, "dm", "cb", 0, 128)
+        tt("V", T.dmv[:], ("dmv",), T.dab[:], ("dab",), T.cp[:], ("cp",), A.mult)
+        tt("V", T.nv[:, 0:128], ("nv", 0, 128), T.sab[:, 0:128], ("sab",), T.dmv[:], ("dmv",), A.add)
+        tt("V", T.nv[:, 128:256], ("nv", 128, 256), T.sab[:, 128:256], ("sab",), T.dmv[:], ("dmv",), A.subtract)
+        for s in range(2):
+            tt("V", T.of[:, 8 * s:8 * s + 8], ("of", 8 * s, 8 * s + 8), T.b3[:, 0:8], ("b3",), T.pd[:, 8 * s:8 * s + 8], ("pd",), A.mult)
+        tt("V", T.og[:], ("og",), T.of[:], ("of",), T.dumc[:], ("dumc",), A.add)
+        cpy(T.ofl[:], ("ofl",), T.og[:], ("og",))
+        out = T.pw[:, 0:3 * W + 2 * CAP].indirect(T.ofl[:])
+        op("V", lambda e: e.tensor_copy(out, T.nv[:]), [("nv",), ("ofl",)], [("pw",)], None, 1.0)
+        if not last:
+            for i in range(NT):
+                for k in range(2):
+                    dma("Y", T.inf[2 * i + k::16, :], ("inf", 0, W, 2 * i + k), T.pw[k::16, W * i:W * i + W], ("pw", W * i, W * i + W, k), "d_rb")
+            return
+        dma("Y", T.yh[:], ("yh",), T.pw[0::16, 0:3 * W], ("pw", 0, 3 * W, 0), "d_y1")
+        dma("Y", T.yl[:], ("yl",), T.pw[1::16, 0:3 * W], ("pw", 0, 3 * W, 1), "d_y1")
+        parts = [(384 * i, 384 * i + 384, ("b3", "b6", "b7")[i]) for i in range(NT)]
+        for a, b, bank in parts:
+            mm(T[bank][:, 0:384], bank, T.idb[:], ("idb",), T.yh[:, a:b], ("yh",), True, False)
+            mm(T[bank][:, 0:384], bank, T.idb[:], ("idb",), T.yl[:, a:b], ("yl",), False, True)
+        for n, (a, b, bank) in enumerate(parts):
+            if n == 1:
+                act(T.yf[:, a:b], ("yf", a, b), T[bank][:, 0:384], (bank,), AF.Copy)
+            else:
+                cpy(T.yf[:, a:b], ("yf", a, b), T[bank][:, 0:384], (bank,))
+        dma("Y", T.yn[:], None, T.yf[:], ("yf",), "d_yn1")
+
+    def cursors(last):
+        for be in range(2):
+            for h in range(4):
+                act(T.ltc[:, 24 * be:24 * be + 24, h, :], ("ltc", 384 * be, 384 * be + 384, h), T["st%d" % be][:, 96:192], ("st%d" % be,), AF.Copy, scale=co[:, h:h + 1], extra=[("cols", h, h + 1)])
+        for be in range(2):
+            for i in range(NT):
+                n = 3 * be + i
+                mm(T.b5[:, 64 * i + 32 * be:64 * i + 32 * be + 32], "b5", T.ltc[:, 8 * n:8 * n + 8, :, :], ("ltc", 384 * be, 384 * be + 384), T.sel[:], ("sel",), True, True)
+        cpy(T.ci[:], ("ci",), T.b5[:, 0:192], ("b5",))
+        ts(T.cj[:], ("cj",), T.ci[:], ("ci",), STAMP - 1, None, A.bitwise_and)
+        if last:
+            cpy(T.ycf[:], ("ycf",), T.cj[:], ("cj",))
+            dma("Y", T.yc[:], None, T.ycf[:], ("ycf",), "d_yc")
+        else:
+            cpy(T.lst[:], ("lst",), T.cj[:], ("cj",))
+
+    def pull(t, last):
+        diag("b4", 64, 128, "df", "ra", 0, K)
+        cpy(T.kl[:], ("kl",), T.b4[:, 64:128], ("b4",))
+        xn = "x%d" % (t + 1)
+        for be in range(2):
+            a, b = H * be, H * be + H
+            ysrc = T[xn][:, 0:W].indirect(T.kl[:, 32 * be:32 * be + 32])
+            op("V", lambda e, ysrc=ysrc, a=a, b=b: e.tensor_tensor(T.dd[:, a:b], ysrc, T.wf[:, a:b], A.subtract), [(xn,), ("kl",), ("wf", a, b)], [("dd", a, b)], None, us(1.5 * H))
+            D, dn = T["b%d" % be], "b%d" % be
+            ts(D[:], (dn,), T.dd[:, a:b], ("dd", a, b), 8.0, -8.0, A.min, A.max)
+            tt("V", T.wf[:, a:b], ("wf", a, b), D[:], (dn,), T.wf[:, a:b], ("wf", a, b), A.add)
+            if last:
+                dma("S", T.yw[:, a:b], None, T.wf[:, a:b], ("wf", a, b), "d_yw%d" % be)
+
+    types_in()
+    for t in range(ROUNDS):
+        last = t == ROUNDS - 1
+        streams = [(record(finds, 0), 0.0), (record(finds, 1), FB)]
+        if t == 0:
+            streams.append((record(later), LB))
+        merge(*streams)
+        places()
+        merge((record(swap, last), 0.0), (record(cursors, last), CB), (record(pull, t, last), PB))
+    for s in sorted(total):
+        know("G", s, total[s])

@@ -5,10 +5,11 @@ AF = ActivationFunctionType
 W, K, NT, ROUNDS, FINDS, CAP = 6144, 1024, 3, 2, 8, 128
 H = K // 2
 STAMP = 8192
-BIG = 1 << 17
+BIG = 1 << 18
 NEQ = 4
 MS = 3
-FB, CB, PB, LB = 0.05, 0.3, 0.8, 0.15
+FB, CB, PB, LB = 0.0, 0.3, 0.4, 0.4
+WP = 0.001
 SB, BF, FP, I32, U16 = "sbuf", "bfloat16", "float32", "int32", "uint16"
 SCRATCH = {
     "xs": (SB, [128, W], BF), "x1": (SB, [128, W], BF), "x2": (SB, [128, W], BF),
@@ -19,18 +20,17 @@ SCRATCH = {
     "f32": (SB, [128, 384], I32), "fhi": (SB, [128, 384], BF), "flo": (SB, [128, 384], BF),
     "pv": (SB, [128, 1152], FP), "phi": (SB, [128, 1152], BF), "plo": (SB, [128, 1152], BF),
     "cur32": (SB, [128, 192], I32), "typ32": (SB, [128, 64], I32), "tf": (SB, [128, 64], FP),
-    "lst": (SB, [128, 192], U16), "ci": (SB, [128, 192], I32), "cj": (SB, [128, 192], I32), "ycf": (SB, [128, 192], FP),
+    "lst": (SB, [128, 192], U16), "ci": (SB, [128, 384], I32), "ycf": (SB, [128, 192], FP),
     "ones": (SB, [128, 192], BF), "idf": (SB, [128, 8, 4, 4], FP), "idb": (SB, [128, 128], BF), "idn": (SB, [128, 8 * 128], BF),
-    "stl": (SB, [128, 128 * (FINDS + 1)], BF), "c72": (SB, [128, 128], BF),
+    "stl": (SB, [128, 128 * (ROUNDS * FINDS + 1)], BF), "c72": (SB, [128, 128], BF),
     "wnx": (SB, [128, 24], BF), "wv": (SB, [128, 24], BF), "wx": (SB, [128, 48], BF), "wbit": (SB, [128, 24], BF), "wcnt": (SB, [128, 48], BF),
     "sel": (SB, [128, 32], FP), "selr": (SB, [128, 32], FP),
     "pid": (SB, [128, 1], I32), "pm": (SB, [128, 4], I32), "cols": (SB, [128, 16], FP),
-    "bo": (SB, [128, 128], BF), "lm": (SB, [128, 128], BF), "plw": (SB, [128, 128], BF),
-    "eqm": (SB, [128, 16, 8, 16], BF), "dm": (SB, [128, 16, 8, 16], BF), "dp": (SB, [128, 16, 8, 16], BF),
-    "db": (SB, [128, 16, 8, 16], BF), "df": (SB, [128, 16, 8, 16], BF),
+    "bo": (SB, [128, 128], BF), "lm": (SB, [128, 128], BF), "plw": (SB, [128, 128], BF), "km": (SB, [128, 128], BF),
+    "eqm": (SB, [128, 16, 8, 16], BF), "dp": (SB, [128, 16, 8, 16], BF), "db": (SB, [128, 16, 8, 16], BF), "df": (SB, [128, 16, 8, 16], BF),
     "kc": (SB, [128, 8], FP), "kch": (SB, [128, 8], FP), "dumc": (SB, [128, 16], FP), "kio": (SB, [128, 128], FP),
-    "ttl": (SB, [128, 256], FP), "eq": (SB, [128, 256 * NEQ], BF),
-    "mz": (SB, [128, 128], FP), "mzi": (SB, [128, 128], I32), "mzj": (SB, [128, 128], I32), "mp4": (SB, [128, 32, 4], FP),
+    "ttl": (SB, [128, 256], FP), "eq": (SB, [128, 256 * NEQ], BF), "lk": (SB, [128, 128], BF),
+    "mz": (SB, [128, 128], FP), "mzi": (SB, [128, 256], I32), "mp4": (SB, [128, 32, 4], FP),
     "lte": (SB, [128, 32, 4, 4], FP), "ltc": (SB, [128, 48, 4, 4], FP),
     "ot": (SB, [128, 128], U16), "otf": (SB, [128, 64], FP), "nq": (SB, [128, 64], BF),
     "ra": (SB, [128, K + 16], BF), "rb": (SB, [128, K + 16], BF),
@@ -38,13 +38,13 @@ SCRATCH = {
     "ck": (SB, [128, 8], FP), "ckl": (SB, [128, 8], U16), "ckb": (SB, [128, 8], BF), "le": (SB, [128, 128], BF), "jk": (SB, [128, 8], U16),
     "sab": (SB, [128, 256], BF), "plr": (SB, [128, 256], U16), "plt": (SB, [128, 16], FP),
     "cb": (SB, [128, 128], BF), "cp": (SB, [128, 128], FP), "dab": (SB, [128, 128], FP), "dmv": (SB, [128, 128], FP),
-    "nv": (SB, [128, 256], BF), "pd": (SB, [128, 16], FP), "of": (SB, [128, 16], FP), "og": (SB, [128, 16], FP), "ofl": (SB, [128, 16], U16),
+    "nv": (SB, [128, 256], BF), "pd": (SB, [128, 16], FP), "of": (SB, [128, 32], FP), "ofl": (SB, [128, 16], U16),
     "kl": (SB, [128, 64], U16), "yh": (SB, [128, 1152], BF), "yl": (SB, [128, 1152], BF), "yf": (SB, [128, 1152], FP),
 }
 for _b in range(2):
     for _n, _s, _d in (("ge", [128, H], BF), ("rw", [128, H], BF), ("off", [128, 32], U16), ("st", [128, 192], FP), ("gt", [128, 192], BF),
-                       ("sg", [128, 192], BF), ("ab", [128, 96], FP), ("tt", [128, 96], FP), ("tu", [128, 32], FP), ("mp", [128, 8, 4], FP),
-                       ("lt", [128, 8, 4, 4], FP), ("oi", [128, 32], I32), ("oj", [128, 32], I32)):
+                       ("sg", [128, 192], BF), ("ab", [128, 96], BF), ("ac", [128, 96], FP), ("tt", [128, 96], FP),
+                       ("tu", [128, 32], FP), ("mp", [128, 8, 4], FP), ("lt", [128, 8, 4, 4], FP), ("oi", [128, 32], I32), ("oj", [128, 32], I32)):
         SCRATCH["%s%d" % (_n, _b)] = (SB, _s, _d)
 for _i in range(8):
     SCRATCH["b%d" % _i] = ("psum", [128, 512], FP)
@@ -146,9 +146,11 @@ def rank_program(g, core, T, topo):
         while True:
             best = None
             for x in st:
-                if x[1] < len(x[0]):
+                if x[1] < len(x[0]) and x[0][x[1]] is None and all(y[1] == len(y[0]) for y in st[2:]):
+                    x[1] += 1
+                if x[1] < len(x[0]) and x[0][x[1]] is not None:
                     o = x[0][x[1]]
-                    t = needs(o[0], o[2], o[3], o[4])[1] + x[2]
+                    t = needs(o[0], o[2], o[3], o[4])[1] + x[2] + WP * x[1]
                     if best is None or t < best[0]:
                         best = (t, x)
             if best is None:
@@ -229,14 +231,17 @@ def rank_program(g, core, T, topo):
     fill("wbit", 16.0)
     fill("idf", 1.0)
     fill("sel", 1.0)
-    for t in range(FINDS + 1):
-        fill("stl", float(BIG // 128) if t == 0 else float(STAMP // 128 * t), 128 * t, 128 * t + 128)
+
+    def stamp(t):
+        fill("stl", (BIG if t == 0 else STAMP * t) / 128.0, 128 * t, 128 * t + 128)
+
+    for t in range(5):
+        stamp(t)
+    fill("bo", 1.0)
     for be in range(2):
         fill("gt%d" % be, 0.0, 96, 192)
-    fill("bo", 1.0)
-    fill("eqm", 1.0)
     op("G", lambda e: e.iota(T.pid[:], [[1, 1]], 0, 1), [], [("pid",)])
-    op("G", lambda e: e.iota(T.pv[:], [[W, 3], [1, 384]], 0, 384, allow_small_or_imprecise_dtypes=True), [], [("pv",)])
+    op("G", lambda e: e.iota(T.pv[:, 0:384], [[1, 384]], 0, 384, allow_small_or_imprecise_dtypes=True), [], [("pv", 0, 384)])
     aff("idf", "idf", [[-1, 128]], A.is_equal, 0, 1)
     aff("sel", "sel", [[-4, 32]], A.is_ge, 0, 1)
     aff("sel", "sel", [[4, 32]], A.is_ge, 3, -1)
@@ -246,6 +251,7 @@ def rank_program(g, core, T, topo):
     aff("wv", "wv", [[0, 3], [16, 8]], A.is_ge, 10, -1)
     aff("wcnt", "wcnt", [[0, 6], [-16, 8]], A.is_ge, 0, 1)
     aff("wcnt", "wcnt", [[0, 6], [16, 8]], A.is_ge, 15, -1)
+    op("G", lambda e: e.iota(T.pv[:, 384:1152], [[W, 2], [1, 384]], W, 384, allow_small_or_imprecise_dtypes=True), [], [("pv", 384, 1152)])
     aff("wbit", "wbit", [[-1, 3], [-16, 8]], A.is_equal, -6, 1)
     pm, co = T.pm, T.cols
     ts(pm[:, 0:1], ("pm", 0, 1), T.pid[:], ("pid",), 3, None, A.bitwise_and)
@@ -256,8 +262,6 @@ def rank_program(g, core, T, topo):
         ts(co[:, h:h + 1], ("cols", h, h + 1), pm[:, 0:1], ("pm", 0, 1), h, None, A.is_equal)
         ts(co[:, 4 + h:5 + h], ("cols", 4 + h, 5 + h), pm[:, 1:2], ("pm", 1, 2), h, None, A.is_equal)
     ts(co[:, 9:10], ("cols", 9, 10), pm[:, 3:4], ("pm", 3, 4), -W, None, A.mult)
-    ts(co[:, 10:11], ("cols", 10, 11), pm[:, 2:3], ("pm", 2, 3), 2, None, A.is_lt)
-    ts(co[:, 11:12], ("cols", 11, 12), pm[:, 3:4], ("pm", 3, 4), -16, None, A.mult)
 
     def split(hi, lo, src, n0, n1, scalar=False):
         if scalar:
@@ -272,14 +276,14 @@ def rank_program(g, core, T, topo):
     def to_pw(k, i, src, n0):
         dma("Y", T.pw[k::16, W * i:W * i + W], ("pw", W * i, W * i + W, k), T[src][:, n0:n0 + 384], (src, n0, n0 + 384), "d_pw")
 
-    act(T.pv[:], ("pv",), T.pv[:], ("pv",), AF.Identity, bias=co[:, 9:10], extra=[("cols", 9, 10)])
-    split("phi", "plo", "pv", 0, 384, True)
-    to_inf(9, "phi", 0)
-    to_inf(10, "plo", 0)
+    act(T.pv[:, 0:384], ("pv", 0, 384), T.pv[:, 0:384], ("pv", 0, 384), AF.Identity, bias=co[:, 9:10], extra=[("cols", 9, 10)])
     for i in range(NT):
         split("nhi", "nlo", "n32", 384 * i, 384 * i + 384)
         to_inf(2 * i, "nhi", 384 * i)
         to_inf(2 * i + 1, "nlo", 384 * i)
+    split("phi", "plo", "pv", 0, 384, True)
+    to_inf(9, "phi", 0)
+    to_inf(10, "plo", 0)
     ts(T.mi[:, 0:384], ("mi", 0, 384), T.m32[:], ("m32",), 1, None, A.bitwise_and)
     ts(T.mi[:, 384:768], ("mi", 384, 768), T.m32[:], ("m32",), 2, None, A.bitwise_and)
     ts(T.bits[:, 768:1152], ("bits", 768, 1152), T.m32[:], ("m32",), 4, None, A.is_ge)
@@ -293,13 +297,16 @@ def rank_program(g, core, T, topo):
     cpy(T.lst[:], ("lst",), T.cur32[:], ("cur32",))
     cpy(T.tf[:], ("tf",), T.typ32[:], ("typ32",))
     cpy(T.idb[:], ("idb",), T.idf[:], ("idf",))
-    for n, v in enumerate((16.0, 0.5, -0.5, -1.0, float(BIG), W / 2.0, float(W), float(4 * BIG))):
+    for n, v in enumerate((16.0, 0.5, -0.5, -1.0, float(BIG), W / 2.0, float(W), float(BIG))):
         ts(T.idn[:, 128 * n:128 * n + 128], ("idn", 128 * n, 128 * n + 128), T.idb[:], ("idb",), v, None, A.mult)
     tt("V", T.selr[:], ("selr",), T.idf[:, :, 0, :], ("idf",), T.idf[:, :, 1, :], ("idf",), A.add)
     for h in (2, 3):
         tt("V", T.selr[:], ("selr",), T.selr[:], ("selr",), T.idf[:, :, h, :], ("idf",), A.add)
     cpy(T.wx[:, 0:24], ("wx", 0, 24), T.wnx[:], ("wnx",))
     cpy(T.wx[:, 24:48], ("wx", 24, 48), T.wv[:], ("wv",))
+    for t in range(5, ROUNDS * FINDS + 1):
+        stamp(t)
+    fill("c72", 1.5 * W / 128)
 
     aff("bo", "bo", [[-16, 8], [0, 16]], A.is_ge, 0, 1)
     aff("bo", "bo", [[16, 8], [0, 16]], A.is_ge, 15, -1)
@@ -308,6 +315,7 @@ def rank_program(g, core, T, topo):
     aff("lm", "bo", [[-1, 128]], A.is_gt, 0, 1)
     op("G", lambda e: e.iota(T.kc[:], [[16, 8]], 0, 1, allow_small_or_imprecise_dtypes=True), [], [("kc",)])
     op("G", lambda e: e.iota(T.kio[:], [[1, 128]], 0, 0, allow_small_or_imprecise_dtypes=True), [], [("kio",)])
+    op("G", lambda e: e.iota(T.km[:], [[0, 8], [1, 16]], 0, 0, allow_small_or_imprecise_dtypes=True), [], [("km",)])
 
     know("G", "l_x", total["l_x"])
     total["tx"] = 0
@@ -320,16 +328,16 @@ def rank_program(g, core, T, topo):
         total[rx] = len(topo.engines(src, core))
         acc[buf] = [(0, 1 << 20, None, "R", rx, total[rx], True)]
 
+    fill("eqm", 1.0)
     aff("eqm", "eqm", [[1, 16], [0, 8], [-1, 16]], A.is_equal, 0, 0)
     aff("db", "eqm", [[0, 16], [-16, 8], [0, 16]], A.is_equal, -4, 1)
     aff("df", "eqm", [[0, 16], [-16, 8], [0, 16]], A.is_ge, -5, 1)
     aff("df", "df", [[0, 16], [16, 8], [0, 16]], A.is_ge, 6, -1)
-    aff("dm", "eqm", [[0, 16], [-16, 8], [0, 16]], A.is_ge, 0, 1)
-    aff("dm", "dm", [[0, 16], [16, 8], [0, 16]], A.is_ge, 15, -1)
     aff("dp", "eqm", [[0, 16], [-16, 8], [0, 16]], A.is_ge, -2, 1)
     aff("dp", "dp", [[0, 16], [16, 8], [0, 16]], A.is_ge, 3, -1)
 
     def later():
+        act(T.pv[:, 384:1152], ("pv", 384, 1152), T.pv[:, 384:1152], ("pv", 384, 1152), AF.Identity, bias=co[:, 9:10], extra=[("cols", 9, 10)])
         for i in range(1, NT):
             split("phi", "plo", "pv", 384 * i, 384 * i + 384, True)
         split("fhi", "flo", "f32", 0, 384)
@@ -339,12 +347,15 @@ def rank_program(g, core, T, topo):
         for i in range(NT):
             for k in range(7, 16):
                 dma("Y", T.pw[k::16, W * i:W * i + W], ("pw", W * i, W * i + W, k), T.x[k::16, :], None, "d_pf")
+        cpy(co[:, 8:9], ("cols", 8, 9), pm[:, 2:3], ("pm", 2, 3))
+        ts(co[:, 10:11], ("cols", 10, 11), pm[:, 2:3], ("pm", 2, 3), 2, None, A.is_lt)
+        ts(co[:, 11:12], ("cols", 11, 12), pm[:, 3:4], ("pm", 3, 4), -16, None, A.mult)
         ts(T.kc[:], ("kc",), T.kc[:], ("kc",), co[:, 11:12], None, A.add, extra=[("cols", 11, 12)])
+        ts(T.km[:], ("km",), T.km[:], ("km",), co[:, 8:9], None, A.is_equal, extra=[("cols", 8, 9)])
         ts(T.kch[:], ("kch",), T.kc[:], ("kc",), 0.5, None, A.add)
         ts(T.dumc[:, 0:8], ("dumc", 0, 8), T.kc[:], ("kc",), 3 * W, None, A.add)
         ts(T.dumc[:, 8:16], ("dumc", 8, 16), T.kc[:], ("kc",), 3 * W + CAP, None, A.add)
         ts(T.lm[:], ("lm",), T.lm[:], ("lm",), -1.0, None, A.mult)
-        fill("c72", 1.5 * W / 128)
         fill("rt", 65536.0, 64, 72)
         fill("ra", 16384.0, K, K + 16)
         fill("rb", 16384.0, K, K + 16)
@@ -363,21 +374,21 @@ def rank_program(g, core, T, topo):
                 ts(T.ttl[:, 128 * be + h:128 * be + 128:4], ("ttl", 128 * be, 128 * be + 128, h), T.tf[:, 32 * be:32 * be + 32], ("tf",), co[:, 4 + h:5 + h], None, A.mult, extra=[("cols", 4 + h, 5 + h)])
             O, ob = T["b%d" % (6 + be)], "b%d" % (6 + be)
             mm(O[:, 0:32], ob, T.ttl[:, 128 * be:128 * be + 128], ("ttl", 128 * be, 128 * be + 128), T.selr[:], ("selr",), True, True)
-            ab, gt = "ab%d" % be, "gt%d" % be
+            ac, gt = "ac%d" % be, "gt%d" % be
             for i in range(NT):
-                act(T[ab][:, 32 * i:32 * i + 32], (ab, 32 * i, 32 * i + 32), O[:, 0:32], (ob,), AF.Abs, bias=-float(i))
-            act(T[gt][:, 0:96], (gt, 0, 96), T[ab][:], (ab,), AF.Sign, bias=0.5, scale=-1.0)
+                act(T[ac][:, 32 * i:32 * i + 32], (ac, 32 * i, 32 * i + 32), O[:, 0:32], (ob,), AF.Abs, bias=-float(i))
+            act(T[gt][:, 0:96], (gt, 0, 96), T[ac][:], (ac,), AF.Sign, bias=0.5, scale=-1.0)
 
-    def pick(be, s0):
-        st, gt, t, u = T["st%d" % be], T["gt%d" % be], T["tt%d" % be], T["tu%d" % be]
+    def pick(be, s0, own="gt%d"):
+        st, t, u = T["st%d" % be], T["tt%d" % be], T["tu%d" % be]
         P, pb = T["b%d" % (4 + be)], "b%d" % (4 + be)
-        mm(P[:, 128:224], pb, *IPEN, gt[:, 0:96], ("gt%d" % be, 0, 96), True, True)
+        mm(P[:, 128:224], pb, *IPEN, T[own % be][:, 0:96], (own % be, 0, 96), True, True)
         tt("V", t[:], ("tt%d" % be,), P[:, 128:224], (pb,), st[:, s0:s0 + 96], ("st%d" % be, s0, s0 + 96), A.add)
         tt("V", u[:], ("tu%d" % be,), t[:, 0:32], ("tt%d" % be,), t[:, 32:64], ("tt%d" % be,), A.max)
 
-    def next_list(be, more=None):
+    def next_list(be, more=None, own="gt%d"):
         t, u, mp, lt = T["tt%d" % be], T["tu%d" % be], T["mp%d" % be], T["lt%d" % be]
-        pick(be, 0)
+        pick(be, 0, own)
         tt("V", mp[:], ("mp%d" % be,), u[:], ("tu%d" % be,), t[:, 64:96], ("tt%d" % be,), A.max)
         masks(lambda h: lt[:, :, h, :], "lt%d" % be, 0, 128, mp[:], ("mp%d" % be,), MS)
         if more:
@@ -389,17 +400,26 @@ def rank_program(g, core, T, topo):
         ts(T[oj][:], (oj,), T[oi][:], (oi,), STAMP - 1, None, A.bitwise_and)
         cpy(T[off][:], (off,), T[oj][:], (oj,))
 
-    def round_start(be):
+    def round_start(be, t):
         X, xb, st = T["b%d" % be], "b%d" % be, "st%d" % be
-        mm(X[:, 0:192], xb, T.stl[:, 0:128], ("stl",), T.ones[:], ("ones",), True, False)
+        n = 96 if t else 192
+        mm(X[:, 0:n], xb, T.stl[:, 0:128], ("stl", 0, 128), T.ones[:, 0:n], ("ones",), True, False)
         for i in range(NT):
             buf = ("rw%d" if i % 2 == 0 else "ge%d") % be
             l0 = 64 * i + 32 * be
-            gather("S" if (i + be) % 2 == 0 else "V", T[buf][:], (buf,), T.inf, "inf", 0, W, T.lst[:, l0:l0 + 32], ("lst",))
+            q = "S" if (i + be) % 2 == 0 else "V"
+            lst = (T.lst[:, l0:l0 + 32], ("lst",))
+            if t:
+                gather(q, T[buf][:], (buf,), T.pw, "pw", 0, 3 * W, *lst)
+            else:
+                gather(q, T[buf][:], (buf,), T.inf, "inf", 0, W, *lst)
             for b in range(4):
-                mm(X[:, 32 * i + b:32 * i + 32:4], xb, T[buf][:, b::4], (buf,), T.wx[:, 8 * i:8 * i + 8], ("wx",), False, False)
-                mm(X[:, 96 + 32 * i + b:128 + 32 * i:4], xb, T[buf][:, b::4], (buf,), T.wx[:, 24 + 8 * i:32 + 8 * i], ("wx",), False, i == NT - 1 and b == 3)
-        cpy(T[st][:], (st,), X[:, 0:192], (xb,))
+                end = i == NT - 1 and b == 3
+                w0 = 0 if t else 8 * i
+                mm(X[:, 32 * i + b:32 * i + 32:4], xb, T[buf][:, b::4], (buf,), T.wx[:, w0:w0 + 8], ("wx",), False, end and t > 0)
+                if t == 0:
+                    mm(X[:, 96 + 32 * i + b:128 + 32 * i:4], xb, T[buf][:, b::4], (buf,), T.wx[:, 24 + 8 * i:32 + 8 * i], ("wx",), False, end)
+        cpy(T[st][:, 0:n], (st, 0, n), X[:, 0:n], (xb,))
         next_list(be)
 
     def find(be, q, last):
@@ -410,7 +430,7 @@ def rank_program(g, core, T, topo):
         op("V", lambda e: e.tensor_tensor(T[ge][:], src, T.wf[:, H * be:H * be + H], A.is_ge), [("xs",), (off,), ("wf", H * be, H * be + H)], [(ge,)], None, us(1.5 * H))
         gather("S", T[rw][:], (rw,), T.inf, "inf", 0, W, T[off][:], (off,))
         mm(Y[:, 0:192], yb, *I16, T[gt][:], (gt,), True, False)
-        mm(X[:, 0:192], xb, T.stl[:, 128 * (q + 1):128 * (q + 2)], ("stl",), T.ones[:], ("ones",), True, False)
+        mm(X[:, 0:192], xb, T.stl[:, 128 * q:128 * q + 128], ("stl", 128 * q, 128 * q + 128), T.ones[:], ("ones",), True, False)
         mm(Z[:, 0:96], zb, *IH, T[gt][:, 0:96], (gt, 0, 96), True, False)
         mm(Z[:, 0:32], zb, *IMH, T[gt][:, 64:96], (gt, 0, 96), False, False)
         mm(Z[:, 32:96], zb, *IMH, T[gt][:, 0:64], (gt, 0, 96), False, False)
@@ -433,48 +453,54 @@ def rank_program(g, core, T, topo):
         if last:
             cursors_too()
         else:
-            next_list(be, cursors_too)
+            next_list(be, cursors_too, "ab%d")
 
-    def finds(be):
-        round_start(be)
+    def finds(be, t):
+        round_start(be, t)
         for q in range(FINDS):
-            find(be, q, q == FINDS - 1)
+            find(be, FINDS * t + q + 1, q == FINDS - 1)
+        rec[0].append(None)
+        places(be)
 
-    def diag(bank, c0, c1, d, src, s0, s1, start=True, stop=True):
+    def diag(bank, c0, c1, d, src, s0, s1):
         for i in range(16):
-            mm(T[bank][:, c0:c1], bank, T[d][:, i, :, :], (d,), T[src][:, s0 + i:s1:16], (src, s0, s1), start and i == 0, stop and i == 15)
+            mm(T[bank][:, c0:c1], bank, T[d][:, i, :, :], (d,), T[src][:, s0 + i:s1:16], (src, s0, s1), i == 0, i == 15)
 
-    def places():
-        for be in range(2):
-            st, gt, tb, ub, ab, mp = [n % be for n in ("st%d", "gt%d", "tt%d", "tu%d", "ab%d", "mp%d")]
-            pick(be, 96)
-            tt("V", T.mz[:, 32 * be:32 * be + 32], ("mz", 32 * be, 32 * be + 32), T[ub][:], (ub,), T[tb][:, 64:96], (tb,), A.max)
-            tt("V", T[ab][:, 0:32], (ab, 0, 32), T[st][:, 96:128], (st,), T[gt][:, 64:96], (gt, 0, 96), A.mult)
-            tt("V", T[ab][:, 32:96], (ab, 32, 96), T[st][:, 128:192], (st,), T[gt][:, 0:64], (gt, 0, 96), A.mult)
-            tt("V", T[mp][:], (mp,), T[ab][:, 0:32], (ab,), T[ab][:, 32:64], (ab,), A.max)
-            tt("V", T.mz[:, 64 + 32 * be:96 + 32 * be], ("mz", 64 + 32 * be, 96 + 32 * be), T[mp][:], (mp,), T[ab][:, 64:96], (ab,), A.max)
-        mm(T.b6[:, 0:128], "b6", T.c72[:], ("c72",), T.ones[:, 0:128], ("ones",), True, False)
+    def slot_list(bank, src, stop):
+        P = T[bank]
+        mm(P[:, 128:256], bank, T[src][:], (src,), T.bo[:], ("bo",), True, True)
+        tt("V", T.lk[:], ("lk",), P[:, 128:256], (bank,), T.km[:], ("km",), A.mult)
+        mm(P[:, 0:8], bank, T.lk[:], ("lk",), T.bo[:, 0:128:16], ("bo",), True, stop)
+
+    def places(be):
+        st, gt, tb, ub, ac, mp = [n % be for n in ("st%d", "gt%d", "tt%d", "tu%d", "ac%d", "mp%d")]
+        Y, yb, O, ob = T["b%d" % (2 + be)], "b%d" % (2 + be), T["b%d" % (6 + be)], "b%d" % (6 + be)
+        a, b = 64 * be, 64 * be + 64
+        mm(Y[:, 0:64], yb, T.c72[:], ("c72",), T.ones[:, 0:64], ("ones",), True, False)
         for s in range(2):
-            for be in range(2):
-                o = T.b6[:, 64 * s + 32 * be:64 * s + 32 * be + 32]
-                gt = "gt%d" % be
-                mm(o, "b6", *IW1, T[gt][:, 0:32], (gt, 0, 96), False, False)
-                mm(o, "b6", *IW2, T[gt][:, 32:64], (gt, 0, 96), False, s == 1 and be == 1)
-        cpy(T.mzi[:], ("mzi",), T.mz[:], ("mz",))
-        ts(T.mzj[:], ("mzj",), T.mzi[:], ("mzi",), STAMP - 1, None, A.bitwise_and)
-        tt("V", T.mp4[:], ("mp4",), T.b6[:, 0:128], ("b6",), T.mzj[:], ("mzj",), A.add)
-        masks(lambda h: T.lte[:, :, h, :], "lte", 0, 512, T.mp4[:], ("mp4",), 2)
-        for n in range(4):
-            mm(T.b7[:, 32 * n:32 * n + 32], "b7", T.lte[:, 8 * n:8 * n + 8, :, :], ("lte",), T.sel[:], ("sel",), True, True)
-        cpy(T.ot[:], ("ot",), T.b7[:, 0:128], ("b7",))
-        gather("V", T.ra[:, 0:H], ("ra", 0, H), T.pw, "pw", 0, 3 * W, T.ot[:, 0:32], ("ot",))
-        gather("S", T.ra[:, H:K], ("ra", H, K), T.pw, "pw", 0, 3 * W, T.ot[:, 32:64], ("ot",))
-        gather("S", T.rb[:, 256:K], ("rb", 256, K), T.pw, "pw", 0, 3 * W, T.ot[:, 80:128], ("ot",))
-        gather("V", T.rb[:, 0:256], ("rb", 0, 256), T.pw, "pw", 0, 3 * W, T.ot[:, 64:80], ("ot",))
-        cpy(T.otf[:], ("otf",), T.b7[:, 0:64], ("b7",))
-        tt("V", T.nq[:], ("nq",), T.b7[:, 64:128], ("b7",), T.otf[:], ("otf",), A.not_equal)
+            mm(Y[:, 32 * s:32 * s + 32], yb, *IW1, T[gt][:, 0:32], (gt, 0, 96), False, False)
+            mm(Y[:, 32 * s:32 * s + 32], yb, *IW2, T[gt][:, 32:64], (gt, 0, 96), False, s == 1)
+        tt("V", T[ac][:, 0:32], (ac, 0, 32), T[st][:, 96:128], (st,), T[gt][:, 64:96], (gt, 0, 96), A.mult)
+        tt("V", T[ac][:, 32:96], (ac, 32, 96), T[st][:, 128:192], (st,), T[gt][:, 0:64], (gt, 0, 96), A.mult)
+        pick(be, 96)
+        tt("V", T.mz[:, a:a + 32], ("mz", a, a + 32), T[ub][:], (ub,), T[tb][:, 64:96], (tb,), A.max)
+        tt("V", T[mp][:], (mp,), T[ac][:, 0:32], (ac,), T[ac][:, 32:64], (ac,), A.max)
+        tt("V", T.mz[:, a + 32:b], ("mz", a + 32, b), T[mp][:], (mp,), T[ac][:, 64:96], (ac,), A.max)
+        cpy(T.mzi[:, a:b], ("mzi", a, b), T.mz[:, a:b], ("mz", a, b))
+        ts(T.mzi[:, 128 + a:128 + b], ("mzi", 128 + a, 128 + b), T.mzi[:, a:b], ("mzi", a, b), STAMP - 1, None, A.bitwise_and)
+        tt("V", T.mp4[:, 16 * be:16 * be + 16, :], ("mp4", a, b), Y[:, 0:64], (yb,), T.mzi[:, 128 + a:128 + b], ("mzi", 128 + a, 128 + b), A.add)
+        masks(lambda h: T.lte[:, 16 * be:16 * be + 16, h, :], "lte", 256 * be, 256 * be + 256, T.mp4[:, 16 * be:16 * be + 16, :], ("mp4", a, b), 2)
+        for s in range(2):
+            n = 16 * be + 8 * s
+            mm(O[:, 32 * s:32 * s + 32], ob, T.lte[:, n:n + 8, :, :], ("lte", 256 * be, 256 * be + 256), T.sel[:], ("sel",), True, True)
+        cpy(T.ot[:, a:b], ("ot", a, b), O[:, 0:64], (ob,))
+        gather("S" if be else "V", T.ra[:, H * be:H * be + H], ("ra", H * be, H * be + H), T.pw, "pw", 0, 3 * W, T.ot[:, a:a + 32], ("ot", a, b))
+        cpy(T.otf[:, a // 2:b // 2], ("otf", a // 2, b // 2), O[:, 0:32], (ob,))
+        tt("V", T.nq[:, a // 2:b // 2], ("nq", a // 2, b // 2), O[:, 32:64], (ob,), T.otf[:, a // 2:b // 2], ("otf", a // 2, b // 2), A.not_equal)
 
     def swap(last):
+        gather("S", T.rb[:, H:K], ("rb", H, K), T.pw, "pw", 0, 3 * W, T.ot[:, 96:128], ("ot", 64, 128))
+        gather("V", T.rb[:, 0:H], ("rb", 0, H), T.pw, "pw", 0, 3 * W, T.ot[:, 32:64], ("ot", 0, 64))
         diag("b2", 0, 64, "db", "ra", 0, K)
         tt("V", T.wt[:], ("wt",), T.b2[:, 0:64], ("b2",), T.nq[:], ("nq",), A.mult)
         op("V", lambda e: e.tensor_tensor_scan(T.pc[:], T.ones[:, 0:64], T.wt[:], 0.0, A.mult, A.add), [("ones",), ("wt",)], [("pc",)])
@@ -488,7 +514,7 @@ def rank_program(g, core, T, topo):
         src = T.rt[:, 0:72].indirect(T.ckl[:])
         op("V", lambda e: e.tensor_tensor(T.le[:], src, T.kio[:], A.is_le), [("rt",), ("ckl",), ("kio",)], [("le",)])
         ts(T.ckb[:], ("ckb",), T.ck[:], ("ck",), 0.5, 32.0, A.mult, A.add)
-        diag("b2", 0, 8, "dm", "le", 0, 128, True, False)
+        slot_list("b2", "le", False)
         mm(T.b2[:, 0:8], "b2", *I16, T.ckb[:], ("ckb",), False, True)
         cpy(T.jk[:], ("jk",), T.b2[:, 0:8], ("b2",))
         gather("V", T.sab[:, 0:128], ("sab", 0, 128), T.ra, "ra", 0, K + 16, T.jk[:], ("jk",))
@@ -506,14 +532,14 @@ def rank_program(g, core, T, topo):
         tt("V", T.pd[:], ("pd",), T.plt[:], ("plt",), T.dumc[:], ("dumc",), A.subtract)
         ts(T.cb[:], ("cb",), T.b7[:, 0:128], ("b7",), 2.0, 1.0 / 16, A.is_equal, A.mult)
         ts(T.cp[:], ("cp",), T.b7[:, 0:128], ("b7",), 2.0, co[:, 10:11], A.is_equal, A.mult, extra=[("cols", 10, 11)])
-        diag("b3", 0, 8, "dm", "cb", 0, 128)
+        slot_list("b3", "cb", True)
         tt("V", T.dmv[:], ("dmv",), T.dab[:], ("dab",), T.cp[:], ("cp",), A.mult)
-        tt("V", T.nv[:, 0:128], ("nv", 0, 128), T.sab[:, 0:128], ("sab",), T.dmv[:], ("dmv",), A.add)
-        tt("V", T.nv[:, 128:256], ("nv", 128, 256), T.sab[:, 128:256], ("sab",), T.dmv[:], ("dmv",), A.subtract)
         for s in range(2):
             tt("V", T.of[:, 8 * s:8 * s + 8], ("of", 8 * s, 8 * s + 8), T.b3[:, 0:8], ("b3",), T.pd[:, 8 * s:8 * s + 8], ("pd",), A.mult)
-        tt("V", T.og[:], ("og",), T.of[:], ("of",), T.dumc[:], ("dumc",), A.add)
-        cpy(T.ofl[:], ("ofl",), T.og[:], ("og",))
+        tt("V", T.nv[:, 0:128], ("nv", 0, 128), T.sab[:, 0:128], ("sab",), T.dmv[:], ("dmv",), A.add)
+        tt("V", T.of[:, 16:32], ("of", 16, 32), T.of[:, 0:16], ("of", 0, 16), T.dumc[:], ("dumc",), A.add)
+        tt("V", T.nv[:, 128:256], ("nv", 128, 256), T.sab[:, 128:256], ("sab",), T.dmv[:], ("dmv",), A.subtract)
+        cpy(T.ofl[:], ("ofl",), T.of[:, 16:32], ("of", 16, 32))
         out = T.pw[:, 0:3 * W + 2 * CAP].indirect(T.ofl[:])
         op("V", lambda e: e.tensor_copy(out, T.nv[:]), [("nv",), ("ofl",)], [("pw",)], None, 1.0)
         if not last:
@@ -542,13 +568,15 @@ def rank_program(g, core, T, topo):
             for i in range(NT):
                 n = 3 * be + i
                 mm(T.b5[:, 64 * i + 32 * be:64 * i + 32 * be + 32], "b5", T.ltc[:, 8 * n:8 * n + 8, :, :], ("ltc", 384 * be, 384 * be + 384), T.sel[:], ("sel",), True, True)
-        cpy(T.ci[:], ("ci",), T.b5[:, 0:192], ("b5",))
-        ts(T.cj[:], ("cj",), T.ci[:], ("ci",), STAMP - 1, None, A.bitwise_and)
+        cpy(T.ci[:, 0:192], ("ci", 0, 192), T.b5[:, 0:192], ("b5",))
+        ts(T.ci[:, 192:384], ("ci", 192, 384), T.ci[:, 0:192], ("ci", 0, 192), STAMP - 1, None, A.bitwise_and)
         if last:
-            cpy(T.ycf[:], ("ycf",), T.cj[:], ("cj",))
+            cpy(T.ycf[:], ("ycf",), T.ci[:, 192:384], ("ci", 192, 384))
             dma("Y", T.yc[:], None, T.ycf[:], ("ycf",), "d_yc")
         else:
-            cpy(T.lst[:], ("lst",), T.cj[:], ("cj",))
+            for i in range(NT):
+                a, b = 64 * i, 64 * i + 64
+                ts(T.lst[:, a:b], ("lst", a, b), T.ci[:, 192 + a:192 + b], ("ci", 192, 384), W * i, None, A.add)
 
     def pull(t, last):
         diag("b4", 64, 128, "df", "ra", 0, K)
@@ -567,11 +595,10 @@ def rank_program(g, core, T, topo):
     types_in()
     for t in range(ROUNDS):
         last = t == ROUNDS - 1
-        streams = [(record(finds, 0), 0.0), (record(finds, 1), FB)]
+        streams = [(record(finds, 0, t), 0.0), (record(finds, 1, t), FB)]
         if t == 0:
             streams.append((record(later), LB))
         merge(*streams)
-        places()
         merge((record(swap, last), 0.0), (record(cursors, last), CB), (record(pull, t, last), PB))
     for s in sorted(total):
         know("G", s, total[s])

from concourse.mybir import AluOpType, ActivationFunctionType

A = AluOpType
AF = ActivationFunctionType
W, K, NT, ROUNDS, FINDS, CAP = 6144, 1024, 3, 2, 8, 128
H = K // 2
STAMP = 8192
BIG = 1 << 18
NEQ = 4
MS = 3
FB, CB, PB, LB = 0.0, 0.3, 0.4, 0.4
WP = 0.001
SB, BF, FP, I32, U16 = "sbuf", "bfloat16", "float32", "int32", "uint16"
SCRATCH = {
    "xs": (SB, [128, W], BF), "x1": (SB, [128, W], BF), "x2": (SB, [128, W], BF),
    "inf": (SB, [128, W], BF), "pw": (SB, [128, 3 * W + 2 * CAP], BF),
    "wb": (SB, [128, K], BF), "wf": (SB, [128, K], FP), "dd": (SB, [128, K], FP),
    "n32": (SB, [128, 1152], I32), "nhi": (SB, [128, 1152], BF), "nlo": (SB, [128, 1152], BF),
    "m32": (SB, [128, 384], I32), "mi": (SB, [128, 768], I32), "bits": (SB, [128, 1152], BF),
    "f32": (SB, [128, 384], I32), "fhi": (SB, [128, 384], BF), "flo": (SB, [128, 384], BF),
    "pv": (SB, [128, 1152], FP), "phi": (SB, [128, 1152], BF), "plo": (SB, [128, 1152], BF),
    "cur32": (SB, [128, 192], I32), "typ32": (SB, [128, 64], I32), "tf": (SB, [128, 64], FP),
    "lst": (SB, [128, 192], U16), "ci": (SB, [128, 384], I32), "ycf": (SB, [128, 192], FP),
    "ones": (SB, [128, 192], BF), "idf": (SB, [128, 8, 4, 4], FP), "idb": (SB, [128, 128], BF), "idn": (SB, [128, 8 * 128], BF),
    "stl": (SB, [128, 128 * (ROUNDS * FINDS + 1)], BF), "c72": (SB, [128, 128], BF),
    "wnx": (SB, [128, 24], BF), "wv": (SB, [128, 24], BF), "wx": (SB, [128, 48], BF), "wbit": (SB, [128, 24], BF), "wcnt": (SB, [128, 48], BF),
    "sel": (SB, [128, 32], FP), "selr": (SB, [128, 32], FP),
    "pid": (SB, [128, 1], I32), "pm": (SB, [128, 4], I32), "cols": (SB, [128, 16], FP),
    "bo": (SB, [128, 128], BF), "lm": (SB, [128, 128], BF), "plw": (SB, [128, 128], BF), "km": (SB, [128, 128], BF),
    "eqm": (SB, [128, 16, 8, 16], BF), "dp": (SB, [128, 16, 8, 16], BF), "db": (SB, [128, 16, 8, 16], BF), "df": (SB, [128, 16, 8, 16], BF),
    "kc": (SB, [128, 8], FP), "kch": (SB, [128, 8], FP), "dumc": (SB, [128, 16], FP), "kio": (SB, [128, 128], FP),
    "ttl": (SB, [128, 256], FP), "eq": (SB, [128, 256 * NEQ], BF), "lk": (SB, [128, 128], BF),
    "mz": (SB, [128, 128], FP), "mzi": (SB, [128, 256], I32), "mp4": (SB, [128, 32, 4], FP),
    "lte": (SB, [128, 32, 4, 4], FP), "ltc": (SB, [128, 48, 4, 4], FP),
    "ot": (SB, [128, 128], U16), "otf": (SB, [128, 64], FP), "nq": (SB, [128, 64], BF),
    "ra": (SB, [128, K + 16], BF), "rb": (SB, [128, K + 16], BF),
    "wt": (SB, [128, 64], BF), "pc": (SB, [128, 64], BF), "rt": (SB, [128, 72], FP), "junk": (SB, [128, 512], BF),
    "ck": (SB, [128, 8], FP), "ckl": (SB, [128, 8], U16), "ckb": (SB, [128, 8], BF), "le": (SB, [128, 128], BF), "jk": (SB, [128, 8], U16),
    "sab": (SB, [128, 256], BF), "plr": (SB, [128, 256], U16), "plt": (SB, [128, 16], FP),
    "cb": (SB, [128, 128], BF), "cp": (SB, [128, 128], FP), "dab": (SB, [128, 128], FP), "dmv": (SB, [128, 128], FP),
    "nv": (SB, [128, 256], BF), "pd": (SB, [128, 16], FP), "of": (SB, [128, 32], FP), "ofl": (SB, [128, 16], U16),
    "kl": (SB, [128, 64], U16), "yh": (SB, [128, 1152], BF), "yl": (SB, [128, 1152], BF), "yf": (SB, [128, 1152], FP),
}
for _b in range(2):
    for _n, _s, _d in (("ge", [128, H], BF), ("rw", [128, H], BF), ("off", [128, 32], U16), ("st", [128, 192], FP), ("gt", [128, 192], BF),
                       ("sg", [128, 192], BF), ("ab", [128, 96], BF), ("ac", [128, 96], FP), ("tt", [128, 96], FP),
                       ("tu", [128, 32], FP), ("mp", [128, 8, 4], FP), ("lt", [128, 8, 4, 4], FP), ("oi", [128, 32], I32), ("oj", [128, 32], I32)):
        SCRATCH["%s%d" % (_n, _b)] = (SB, _s, _d)
for _i in range(8):
    SCRATCH["b%d" % _i] = ("psum", [128, 512], FP)
ENG = {"V": "cv", "S": "cs", "P": "cp_", "G": "cg"}
DMAS = ["l_m", "l_c", "l_t", "l_x", "l_w", "l_f", "d_i0", "d_i1", "d_i2", "d_bi", "d_fl", "d_pf", "d_pw", "d_rb", "d_y1", "d_yc", "d_yw0", "d_yw1", "d_yn1"]
SEMAPHORES = sorted(ENG.values()) + DMAS + ["rx1", "rx2", "tx"]


def rank_program(g, core, T, topo):
    rank = T.rank_of(core)
    if rank is None:
        return
    N = len(T.cores)
    queues = {"V": g.vector, "S": g.scalar, "P": g.tensor, "G": g, "Y": g.sync}
    clock = {q: {} for q in queues}
    total = {}
    snap = {}
    acc = {}
    free = {q: 0.0 for q in queues}
    done = {}
    rec = [None]

    def know(q, sem, val):
        c = clock[q]
        if c.get(sem, 0) >= val:
            return
        queues[q].wait_ge(T.sem[sem], val)
        for s, v in snap.get((sem, val), {}).items():
            if v > c.get(s, 0):
                c[s] = v
        c[sem] = val

    def region(r):
        buf, lo, hi, tag = (r + (0, 1 << 20, None))[:4] if len(r) == 1 else (r + (None,))[:4]
        if SCRATCH.get(buf, ("", 0, 0))[0] == "psum":
            return buf, 0, 512, None, True
        return buf, lo, hi, tag, False

    def needs(q, reads, writes, dma):
        need = {}
        t = free[q]
        for lst, wr in ((reads, False), (writes, True)):
            for r in lst:
                buf, lo, hi, tag, bank = region(r)
                for a in acc.get(buf, ()):
                    if a[1] <= lo or hi <= a[0] or (tag is not None and a[2] is not None and a[2] != tag):
                        continue
                    same = a[3] == q and not dma and a[4] not in DMAS
                    if not (wr or a[6]) and (not bank or same):
                        continue
                    if same and (q == "P" or not a[6]):
                        continue
                    need[a[4]] = max(need.get(a[4], 0), a[5])
                    t = max(t, done.get((a[4], a[5]), 0.0) + 0.06)
        return need, t

    def emit(q, fn, reads, writes, dma, cost):
        need, t = needs(q, reads, writes, dma)
        for s in sorted(need):
            know(q, s, total[s] if s in DMAS else need[s])
        ins = fn(queues[q])
        sem, inc = (dma, 16) if dma else (ENG[q], 1)
        ins.then_inc(T.sem[sem], inc)
        total[sem] = total.get(sem, 0) + inc
        val = total[sem]
        s = dict(clock[q])
        for k2, v2 in snap.get((sem, val - inc), {}).items():
            s[k2] = max(v2, s.get(k2, 0))
        s[sem] = val
        snap[(sem, val)] = s
        free[q] = t + (0.06 if dma else cost)
        done[(sem, val)] = t + (4.0 if dma else cost)
        for lst, wr in ((writes, True), (reads, False)):
            for r in lst:
                buf, lo, hi, tag, bank = region(r)
                keep = []
                for a in acc.get(buf, []):
                    inside = lo <= a[0] and a[1] <= hi and (tag is None or tag == a[2])
                    if inside and (wr or (not a[6] and a[3] == q and a[4] == sem)):
                        continue
                    keep.append(a)
                keep.append((lo, hi, tag, q, sem, val, wr))
                acc[buf] = keep

    def op(q, fn, reads, writes, dma=None, cost=0.1):
        if rec[0] is not None:
            rec[0].append((q, fn, reads, writes, dma, cost))
        else:
            emit(q, fn, reads, writes, dma, cost)

    def record(f, *args):
        rec[0] = []
        f(*args)
        r, rec[0] = rec[0], None
        return r

    def merge(*streams):
        st = [[s, 0, b] for s, b in streams]
        while True:
            best = None
            for x in st:
                if x[1] < len(x[0]) and x[0][x[1]] is None and all(y[1] == len(y[0]) for y in st[2:]):
                    x[1] += 1
                if x[1] < len(x[0]) and x[0][x[1]] is not None:
                    o = x[0][x[1]]
                    t = needs(o[0], o[2], o[3], o[4])[1] + x[2] + WP * x[1]
                    if best is None or t < best[0]:
                        best = (t, x)
            if best is None:
                return
            x = best[1]
            emit(*x[0][x[1]])
            x[1] += 1

    scaled = [(T.idn[:, 128 * n:128 * n + 128], ("idn", 128 * n, 128 * n + 128)) for n in range(8)]
    I16, IH, IMH, IM, IBIG, IW1, IW2, IPEN = scaled

    def cols(ap):
        n = 1
        for d in list(ap.shape)[1:]:
            n *= d
        return n

    def us(cycles):
        return 0.03 + 0.00104 * cycles

    def tt(q, out, o, a, ra, b, rb, f):
        n = cols(out)
        bank = any(region(r)[4] for r in (ra, rb))
        op(q, lambda e: e.tensor_tensor(out, a, b, f), [ra, rb], [o], None, us(max(64, n if bank else 2 * n)))

    def ts(out, o, a, ra, s1, s2, f1, f2=None, extra=()):
        c = us(max(64, cols(out)))
        if f2 is None:
            op("V", lambda e: e.tensor_scalar(out, a, s1, None, f1), [ra] + list(extra), [o], None, c)
        else:
            op("V", lambda e: e.tensor_scalar(out, a, s1, s2, f1, f2), [ra] + list(extra), [o], None, c)

    def cpy(out, o, a, ra):
        op("V", lambda e: e.tensor_copy(out, a), [ra], [o], None, us(max(64, cols(out))))

    def act(out, o, a, ra, f, bias=0.0, scale=1.0, extra=(), accum=None, ao=None):
        c = us(cols(out))
        if accum is None:
            op("S", lambda e: e.activation(out, a, f, bias=bias, scale=scale), [ra] + list(extra), [o], None, c)
        else:
            op("S", lambda e: e.activation(out, a, f, bias=bias, scale=scale, accum_out=accum), [ra] + list(extra), [o, ao], None, c)

    def mm(out, bank, l, rl, r, rr, start, stop):
        op("P", lambda e: e.matmul(out, l, r, start, stop), [rl, rr], [(bank,)], None, max(64, cols(r)) * (0.0024 if rl[0][:2] in ("lt", "tt") else 0.0006))

    def dma(q, out, o, a, ra, sem):
        op(q, lambda e: e.dma_start(out, a), [ra] if ra else [], [o] if o else [], dma=sem)

    def fill(name, v, lo=None, hi=None):
        if lo is None:
            op("V", lambda e: e.memset(T[name][:], v), [], [(name,)])
        else:
            op("V", lambda e: e.memset(T[name][:, lo:hi], v), [], [(name, lo, hi)])

    def aff(out, src, pat, cmp, base, mult):
        op("G", lambda e: e.affine_select(T[out][:], T[src][:], pat, cmp, 0.0, base, mult), [(src,)], [(out,)])

    def gather(q, out, oreg, win, wn, n0, n1, off, offreg):
        src = win[:, n0:n1].indirect(off)
        c = us(1.5 * cols(out))
        if q == "V":
            op("V", lambda e: e.tensor_copy(out, src), [(wn, n0, n1), offreg], [oreg], None, c)
        else:
            op("S", lambda e: e.activation(out, src, AF.Copy), [(wn, n0, n1), offreg], [oreg], None, c)

    for i in range(NT):
        dma("Y", T.n32[:, 384 * i:384 * i + 384], ("n32", 384 * i, 384 * i + 384), T.nxt[:, W * i:W * i + W], None, "d_i%d" % i)
    dma("S", T.m32[:], ("m32",), T.mem[:], None, "l_m")
    dma("S", T.cur32[:], ("cur32",), T.cur[:], None, "l_c")
    dma("S", T.typ32[:], ("typ32",), T.typ[:], None, "l_t")
    dma("S", T.wb[:], ("wb",), T.w0[:], None, "l_w")
    for k in range(11, 16):
        dma("Y", T.inf[k::16, :], ("inf", 0, W, k), T.x[k::16, :], None, "d_fl")

    fill("ones", 1.0)
    for n in ("wnx", "wv", "wcnt"):
        fill(n, 1.0)
    fill("wbit", 16.0)
    fill("idf", 1.0)
    fill("sel", 1.0)

    def stamp(t):
        fill("stl", (BIG if t == 0 else STAMP * t) / 128.0, 128 * t, 128 * t + 128)

    for t in range(5):
        stamp(t)
    fill("bo", 1.0)
    for be in range(2):
        fill("gt%d" % be, 0.0, 96, 192)
    op("G", lambda e: e.iota(T.pid[:], [[1, 1]], 0, 1), [], [("pid",)])
    op("G", lambda e: e.iota(T.pv[:, 0:384], [[1, 384]], 0, 384, allow_small_or_imprecise_dtypes=True), [], [("pv", 0, 384)])
    aff("idf", "idf", [[-1, 128]], A.is_equal, 0, 1)
    aff("sel", "sel", [[-4, 32]], A.is_ge, 0, 1)
    aff("sel", "sel", [[4, 32]], A.is_ge, 3, -1)
    aff("wnx", "wnx", [[-2, 3], [-16, 8]], A.is_ge, 0, 1)
    aff("wnx", "wnx", [[2, 3], [16, 8]], A.is_ge, 1, -1)
    aff("wv", "wv", [[0, 3], [-16, 8]], A.is_ge, -9, 1)
    aff("wv", "wv", [[0, 3], [16, 8]], A.is_ge, 10, -1)
    aff("wcnt", "wcnt", [[0, 6], [-16, 8]], A.is_ge, 0, 1)
    aff("wcnt", "wcnt", [[0, 6], [16, 8]], A.is_ge, 15, -1)
    op("G", lambda e: e.iota(T.pv[:, 384:1152], [[W, 2], [1, 384]], W, 384, allow_small_or_imprecise_dtypes=True), [], [("pv", 384, 1152)])
    aff("wbit", "wbit", [[-1, 3], [-16, 8]], A.is_equal, -6, 1)
    pm, co = T.pm, T.cols
    ts(pm[:, 0:1], ("pm", 0, 1), T.pid[:], ("pid",), 3, None, A.bitwise_and)
    ts(pm[:, 1:2], ("pm", 1, 2), T.pid[:], ("pid",), 2, 3, A.arith_shift_right, A.bitwise_and)
    ts(pm[:, 2:3], ("pm", 2, 3), T.pid[:], ("pid",), 15, None, A.bitwise_and)
    ts(pm[:, 3:4], ("pm", 3, 4), T.pid[:], ("pid",), 4, None, A.arith_shift_right)
    for h in range(4):
        ts(co[:, h:h + 1], ("cols", h, h + 1), pm[:, 0:1], ("pm", 0, 1), h, None, A.is_equal)
        ts(co[:, 4 + h:5 + h], ("cols", 4 + h, 5 + h), pm[:, 1:2], ("pm", 1, 2), h, None, A.is_equal)
    ts(co[:, 9:10], ("cols", 9, 10), pm[:, 3:4], ("pm", 3, 4), -W, None, A.mult)

    def split(hi, lo, src, n0, n1, scalar=False):
        if scalar:
            act(T[hi][:, n0:n1], (hi, n0, n1), T[src][:, n0:n1], (src, n0, n1), AF.Copy)
        else:
            cpy(T[hi][:, n0:n1], (hi, n0, n1), T[src][:, n0:n1], (src, n0, n1))
        tt("V", T[lo][:, n0:n1], (lo, n0, n1), T[src][:, n0:n1], (src, n0, n1), T[hi][:, n0:n1], (hi, n0, n1), A.subtract)

    def to_inf(k, src, n0):
        dma("Y", T.inf[k::16, :], ("inf", 0, W, k), T[src][:, n0:n0 + 384], (src, n0, n0 + 384), "d_bi")

    def to_pw(k, i, src, n0):
        dma("Y", T.pw[k::16, W * i:W * i + W], ("pw", W * i, W * i + W, k), T[src][:, n0:n0 + 384], (src, n0, n0 + 384), "d_pw")

    act(T.pv[:, 0:384], ("pv", 0, 384), T.pv[:, 0:384], ("pv", 0, 384), AF.Identity, bias=co[:, 9:10], extra=[("cols", 9, 10)])
    for i in range(NT):
        split("nhi", "nlo", "n32", 384 * i, 384 * i + 384)
        to_inf(2 * i, "nhi", 384 * i)
        to_inf(2 * i + 1, "nlo", 384 * i)
    split("phi", "plo", "pv", 0, 384, True)
    to_inf(9, "phi", 0)
    to_inf(10, "plo", 0)
    ts(T.mi[:, 0:384], ("mi", 0, 384), T.m32[:], ("m32",), 1, None, A.bitwise_and)
    ts(T.mi[:, 384:768], ("mi", 384, 768), T.m32[:], ("m32",), 2, None, A.bitwise_and)
    ts(T.bits[:, 768:1152], ("bits", 768, 1152), T.m32[:], ("m32",), 4, None, A.is_ge)
    ts(T.bits[:, 0:768], ("bits", 0, 768), T.mi[:], ("mi",), 1, None, A.is_ge)
    for i in range(NT):
        to_inf(6 + i, "bits", 384 * i)
    dma("Y", T.xs[:], ("xs",), T.x[:], None, "l_x")
    act(T.wf[:], ("wf",), T.wb[:], ("wb",), AF.Copy)
    dma("S", T.f32[:], ("f32",), T.fro[:], None, "l_f")

    cpy(T.lst[:], ("lst",), T.cur32[:], ("cur32",))
    cpy(T.tf[:], ("tf",), T.typ32[:], ("typ32",))
    cpy(T.idb[:], ("idb",), T.idf[:], ("idf",))
    for n, v in enumerate((16.0, 0.5, -0.5, -1.0, float(BIG), W / 2.0, float(W), float(BIG))):
        ts(T.idn[:, 128 * n:128 * n + 128], ("idn", 128 * n, 128 * n + 128), T.idb[:], ("idb",), v, None, A.mult)
    tt("V", T.selr[:], ("selr",), T.idf[:, :, 0, :], ("idf",), T.idf[:, :, 1, :], ("idf",), A.add)
    for h in (2, 3):
        tt("V", T.selr[:], ("selr",), T.selr[:], ("selr",), T.idf[:, :, h, :], ("idf",), A.add)
    cpy(T.wx[:, 0:24], ("wx", 0, 24), T.wnx[:], ("wnx",))
    cpy(T.wx[:, 24:48], ("wx", 24, 48), T.wv[:], ("wv",))
    for t in range(5, ROUNDS * FINDS + 1):
        stamp(t)
    fill("c72", 1.5 * W / 128)

    aff("bo", "bo", [[-16, 8], [0, 16]], A.is_ge, 0, 1)
    aff("bo", "bo", [[16, 8], [0, 16]], A.is_ge, 15, -1)
    aff("plw", "bo", [[-16, 8], [0, 16]], A.is_ge, -2, 1)
    aff("plw", "plw", [[16, 8], [0, 16]], A.is_ge, 3, -1)
    aff("lm", "bo", [[-1, 128]], A.is_gt, 0, 1)
    op("G", lambda e: e.iota(T.kc[:], [[16, 8]], 0, 1, allow_small_or_imprecise_dtypes=True), [], [("kc",)])
    op("G", lambda e: e.iota(T.kio[:], [[1, 128]], 0, 0, allow_small_or_imprecise_dtypes=True), [], [("kio",)])
    op("G", lambda e: e.iota(T.km[:], [[0, 8], [1, 16]], 0, 0, allow_small_or_imprecise_dtypes=True), [], [("km",)])

    know("G", "l_x", total["l_x"])
    total["tx"] = 0
    for t, buf in ((0, "x1"), (1, "x2")):
        dst, src = T.cores[(rank - 1 - t) % N], T.cores[(rank + 1 + t) % N]
        rid, pid, _s = topo.addr(dst)
        rx = "rx%d" % (t + 1)
        g.remote_dma(T[buf][:], T.xs[:], T.sem[rx], T.sem.tx, pid, rid, topo.mask(core, dst))
        total["tx"] += len(topo.engines(core, dst))
        total[rx] = len(topo.engines(src, core))
        acc[buf] = [(0, 1 << 20, None, "R", rx, total[rx], True)]

    fill("eqm", 1.0)
    aff("eqm", "eqm", [[1, 16], [0, 8], [-1, 16]], A.is_equal, 0, 0)
    aff("db", "eqm", [[0, 16], [-16, 8], [0, 16]], A.is_equal, -4, 1)
    aff("df", "eqm", [[0, 16], [-16, 8], [0, 16]], A.is_ge, -5, 1)
    aff("df", "df", [[0, 16], [16, 8], [0, 16]], A.is_ge, 6, -1)
    aff("dp", "eqm", [[0, 16], [-16, 8], [0, 16]], A.is_ge, -2, 1)
    aff("dp", "dp", [[0, 16], [16, 8], [0, 16]], A.is_ge, 3, -1)

    def later():
        act(T.pv[:, 384:1152], ("pv", 384, 1152), T.pv[:, 384:1152], ("pv", 384, 1152), AF.Identity, bias=co[:, 9:10], extra=[("cols", 9, 10)])
        for i in range(1, NT):
            split("phi", "plo", "pv", 384 * i, 384 * i + 384, True)
        split("fhi", "flo", "f32", 0, 384)
        for i in range(NT):
            for k, (src, n0) in enumerate((("nhi", 384 * i), ("nlo", 384 * i), ("phi", 384 * i), ("plo", 384 * i), ("bits", 384 * i), ("fhi", 0), ("flo", 0))):
                to_pw(k, i, src, n0)
        for i in range(NT):
            for k in range(7, 16):
                dma("Y", T.pw[k::16, W * i:W * i + W], ("pw", W * i, W * i + W, k), T.x[k::16, :], None, "d_pf")
        cpy(co[:, 8:9], ("cols", 8, 9), pm[:, 2:3], ("pm", 2, 3))
        ts(co[:, 10:11], ("cols", 10, 11), pm[:, 2:3], ("pm", 2, 3), 2, None, A.is_lt)
        ts(co[:, 11:12], ("cols", 11, 12), pm[:, 3:4], ("pm", 3, 4), -16, None, A.mult)
        ts(T.kc[:], ("kc",), T.kc[:], ("kc",), co[:, 11:12], None, A.add, extra=[("cols", 11, 12)])
        ts(T.km[:], ("km",), T.km[:], ("km",), co[:, 8:9], None, A.is_equal, extra=[("cols", 8, 9)])
        ts(T.kch[:], ("kch",), T.kc[:], ("kc",), 0.5, None, A.add)
        ts(T.dumc[:, 0:8], ("dumc", 0, 8), T.kc[:], ("kc",), 3 * W, None, A.add)
        ts(T.dumc[:, 8:16], ("dumc", 8, 16), T.kc[:], ("kc",), 3 * W + CAP, None, A.add)
        ts(T.lm[:], ("lm",), T.lm[:], ("lm",), -1.0, None, A.mult)
        fill("rt", 65536.0, 64, 72)
        fill("ra", 16384.0, K, K + 16)
        fill("rb", 16384.0, K, K + 16)

    def masks(out, obuf, n0, n1, src, sreg, nscalar):
        for h in range(4):
            o = (obuf, n0, n1, h)
            if h < nscalar:
                act(out(h), o, src, sreg, AF.Copy, scale=co[:, h:h + 1], extra=[("cols", h, h + 1)])
            else:
                ts(out(h), o, src, sreg, co[:, h:h + 1], None, A.mult, extra=[("cols", h, h + 1)])

    def types_in():
        for be in range(2):
            for h in range(4):
                ts(T.ttl[:, 128 * be + h:128 * be + 128:4], ("ttl", 128 * be, 128 * be + 128, h), T.tf[:, 32 * be:32 * be + 32], ("tf",), co[:, 4 + h:5 + h], None, A.mult, extra=[("cols", 4 + h, 5 + h)])
            O, ob = T["b%d" % (6 + be)], "b%d" % (6 + be)
            mm(O[:, 0:32], ob, T.ttl[:, 128 * be:128 * be + 128], ("ttl", 128 * be, 128 * be + 128), T.selr[:], ("selr",), True, True)
            ac, gt = "ac%d" % be, "gt%d" % be
            for i in range(NT):
                act(T[ac][:, 32 * i:32 * i + 32], (ac, 32 * i, 32 * i + 32), O[:, 0:32], (ob,), AF.Abs, bias=-float(i))
            act(T[gt][:, 0:96], (gt, 0, 96), T[ac][:], (ac,), AF.Sign, bias=0.5, scale=-1.0)

    def pick(be, s0, own="gt%d"):
        st, t, u = T["st%d" % be], T["tt%d" % be], T["tu%d" % be]
        P, pb = T["b%d" % (4 + be)], "b%d" % (4 + be)
        mm(P[:, 128:224], pb, *IPEN, T[own % be][:, 0:96], (own % be, 0, 96), True, True)
        tt("V", t[:], ("tt%d" % be,), P[:, 128:224], (pb,), st[:, s0:s0 + 96], ("st%d" % be, s0, s0 + 96), A.add)
        tt("V", u[:], ("tu%d" % be,), t[:, 0:32], ("tt%d" % be,), t[:, 32:64], ("tt%d" % be,), A.max)

    def next_list(be, more=None, own="gt%d"):
        t, u, mp, lt = T["tt%d" % be], T["tu%d" % be], T["mp%d" % be], T["lt%d" % be]
        pick(be, 0, own)
        tt("V", mp[:], ("mp%d" % be,), u[:], ("tu%d" % be,), t[:, 64:96], ("tt%d" % be,), A.max)
        masks(lambda h: lt[:, :, h, :], "lt%d" % be, 0, 128, mp[:], ("mp%d" % be,), MS)
        if more:
            more()
        O, ob = T["b%d" % (6 + be)], "b%d" % (6 + be)
        mm(O[:, 0:32], ob, lt[:], ("lt%d" % be,), T.sel[:], ("sel",), True, True)
        oi, oj, off = "oi%d" % be, "oj%d" % be, "off%d" % be
        cpy(T[oi][:], (oi,), O[:, 0:32], (ob,))
        ts(T[oj][:], (oj,), T[oi][:], (oi,), STAMP - 1, None, A.bitwise_and)
        cpy(T[off][:], (off,), T[oj][:], (oj,))

    def round_start(be, t):
        X, xb, st = T["b%d" % be], "b%d" % be, "st%d" % be
        n = 96 if t else 192
        mm(X[:, 0:n], xb, T.stl[:, 0:128], ("stl", 0, 128), T.ones[:, 0:n], ("ones",), True, False)
        for i in range(NT):
            buf = ("rw%d" if i % 2 == 0 else "ge%d") % be
            l0 = 64 * i + 32 * be
            q = "S" if (i + be) % 2 == 0 else "V"
            lst = (T.lst[:, l0:l0 + 32], ("lst",))
            if t:
                gather(q, T[buf][:], (buf,), T.pw, "pw", 0, 3 * W, *lst)
            else:
                gather(q, T[buf][:], (buf,), T.inf, "inf", 0, W, *lst)
            for b in range(4):
                end = i == NT - 1 and b == 3
                w0 = 0 if t else 8 * i
                mm(X[:, 32 * i + b:32 * i + 32:4], xb, T[buf][:, b::4], (buf,), T.wx[:, w0:w0 + 8], ("wx",), False, end and t > 0)
                if t == 0:
                    mm(X[:, 96 + 32 * i + b:128 + 32 * i:4], xb, T[buf][:, b::4], (buf,), T.wx[:, 24 + 8 * i:32 + 8 * i], ("wx",), False, end)
        cpy(T[st][:, 0:n], (st, 0, n), X[:, 0:n], (xb,))
        next_list(be)

    def find(be, q, last):
        ge, rw, off, gt = "ge%d" % be, "rw%d" % be, "off%d" % be, "gt%d" % be
        sg, ab, st = "sg%d" % be, "ab%d" % be, "st%d" % be
        (X, xb), (Y, yb), (Z, zb) = [(T["b%d" % (n + be)], "b%d" % (n + be)) for n in (0, 2, 4)]
        src = T.xs[:, 0:W].indirect(T[off][:])
        op("V", lambda e: e.tensor_tensor(T[ge][:], src, T.wf[:, H * be:H * be + H], A.is_ge), [("xs",), (off,), ("wf", H * be, H * be + H)], [(ge,)], None, us(1.5 * H))
        gather("S", T[rw][:], (rw,), T.inf, "inf", 0, W, T[off][:], (off,))
        mm(Y[:, 0:192], yb, *I16, T[gt][:], (gt,), True, False)
        mm(X[:, 0:192], xb, T.stl[:, 128 * q:128 * q + 128], ("stl", 128 * q, 128 * q + 128), T.ones[:], ("ones",), True, False)
        mm(Z[:, 0:96], zb, *IH, T[gt][:, 0:96], (gt, 0, 96), True, False)
        mm(Z[:, 0:32], zb, *IMH, T[gt][:, 64:96], (gt, 0, 96), False, False)
        mm(Z[:, 32:96], zb, *IMH, T[gt][:, 0:64], (gt, 0, 96), False, False)
        for b in range(4):
            mm(Y[:, b:96:4], yb, T[rw][:, b::4], (rw,), T.wbit[:], ("wbit",), False, False)
        for b in range(4):
            mm(Y[:, b:192:4], yb, T[ge][:, b::4], (ge,), T.wcnt[:], ("wcnt",), False, b == 3)
        for b in range(4):
            mm(X[:, b:192:4], xb, T[rw][:, b::4], (rw,), T.wx[:], ("wx",), False, False)
        act(T[sg][:], (sg,), Y[:, 0:192], (yb,), AF.Sign, bias=-8.5)
        mm(Z[:, 0:96], zb, *IM, T[sg][:, 96:192], (sg,), False, True)
        mm(X[:, 0:96], xb, *IBIG, T[sg][:, 0:96], (sg,), False, False)
        mm(X[:, 96:192], xb, *IBIG, T[sg][:, 0:96], (sg,), False, True)
        act(T[ab][:], (ab,), Z[:, 0:96], (zb,), AF.Abs)
        act(T[gt][:, 0:96], (gt, 0, 96), T[ab][:], (ab,), AF.Sign, bias=-1.5)
        tt("V", T[st][:, 0:96], (st, 0, 96), X[:, 0:96], (xb,), T[st][:, 0:96], (st, 0, 96), A.max)

        def cursors_too():
            tt("V", T[st][:, 96:192], (st, 96, 192), X[:, 96:192], (xb,), T[st][:, 96:192], (st, 96, 192), A.max)
        if last:
            cursors_too()
        else:
            next_list(be, cursors_too, "ab%d")

    def finds(be, t):
        round_start(be, t)
        for q in range(FINDS):
            find(be, FINDS * t + q + 1, q == FINDS - 1)
        rec[0].append(None)
        places(be)

    def diag(bank, c0, c1, d, src, s0, s1):
        for i in range(16):
            mm(T[bank][:, c0:c1], bank, T[d][:, i, :, :], (d,), T[src][:, s0 + i:s1:16], (src, s0, s1), i == 0, i == 15)

    def slot_list(bank, src, stop):
        P = T[bank]
        mm(P[:, 128:256], bank, T[src][:], (src,), T.bo[:], ("bo",), True, True)
        tt("V", T.lk[:], ("lk",), P[:, 128:256], (bank,), T.km[:], ("km",), A.mult)
        mm(P[:, 0:8], bank, T.lk[:], ("lk",), T.bo[:, 0:128:16], ("bo",), True, stop)

    def places(be):
        st, gt, tb, ub, ac, mp = [n % be for n in ("st%d", "gt%d", "tt%d", "tu%d", "ac%d", "mp%d")]
        Y, yb, O, ob = T["b%d" % (2 + be)], "b%d" % (2 + be), T["b%d" % (6 + be)], "b%d" % (6 + be)
        a, b = 64 * be, 64 * be + 64
        mm(Y[:, 0:64], yb, T.c72[:], ("c72",), T.ones[:, 0:64], ("ones",), True, False)
        for s in range(2):
            mm(Y[:, 32 * s:32 * s + 32], yb, *IW1, T[gt][:, 0:32], (gt, 0, 96), False, False)
            mm(Y[:, 32 * s:32 * s + 32], yb, *IW2, T[gt][:, 32:64], (gt, 0, 96), False, s == 1)
        tt("V", T[ac][:, 0:32], (ac, 0, 32), T[st][:, 96:128], (st,), T[gt][:, 64:96], (gt, 0, 96), A.mult)
        tt("V", T[ac][:, 32:96], (ac, 32, 96), T[st][:, 128:192], (st,), T[gt][:, 0:64], (gt, 0, 96), A.mult)
        pick(be, 96)
        tt("V", T.mz[:, a:a + 32], ("mz", a, a + 32), T[ub][:], (ub,), T[tb][:, 64:96], (tb,), A.max)
        tt("V", T[mp][:], (mp,), T[ac][:, 0:32], (ac,), T[ac][:, 32:64], (ac,), A.max)
        tt("V", T.mz[:, a + 32:b], ("mz", a + 32, b), T[mp][:], (mp,), T[ac][:, 64:96], (ac,), A.max)
        cpy(T.mzi[:, a:b], ("mzi", a, b), T.mz[:, a:b], ("mz", a, b))
        ts(T.mzi[:, 128 + a:128 + b], ("mzi", 128 + a, 128 + b), T.mzi[:, a:b], ("mzi", a, b), STAMP - 1, None, A.bitwise_and)
        tt("V", T.mp4[:, 16 * be:16 * be + 16, :], ("mp4", a, b), Y[:, 0:64], (yb,), T.mzi[:, 128 + a:128 + b], ("mzi", 128 + a, 128 + b), A.add)
        masks(lambda h: T.lte[:, 16 * be:16 * be + 16, h, :], "lte", 256 * be, 256 * be + 256, T.mp4[:, 16 * be:16 * be + 16, :], ("mp4", a, b), 2)
        for s in range(2):
            n = 16 * be + 8 * s
            mm(O[:, 32 * s:32 * s + 32], ob, T.lte[:, n:n + 8, :, :], ("lte", 256 * be, 256 * be + 256), T.sel[:], ("sel",), True, True)
        cpy(T.ot[:, a:b], ("ot", a, b), O[:, 0:64], (ob,))
        gather("S" if be else "V", T.ra[:, H * be:H * be + H], ("ra", H * be, H * be + H), T.pw, "pw", 0, 3 * W, T.ot[:, a:a + 32], ("ot", a, b))
        cpy(T.otf[:, a // 2:b // 2], ("otf", a // 2, b // 2), O[:, 0:32], (ob,))
        tt("V", T.nq[:, a // 2:b // 2], ("nq", a // 2, b // 2), O[:, 32:64], (ob,), T.otf[:, a // 2:b // 2], ("otf", a // 2, b // 2), A.not_equal)

    def swap(last):
        gather("S", T.rb[:, H:K], ("rb", H, K), T.pw, "pw", 0, 3 * W, T.ot[:, 96:128], ("ot", 64, 128))
        gather("V", T.rb[:, 0:H], ("rb", 0, H), T.pw, "pw", 0, 3 * W, T.ot[:, 32:64], ("ot", 0, 64))
        diag("b2", 0, 64, "db", "ra", 0, K)
        tt("V", T.wt[:], ("wt",), T.b2[:, 0:64], ("b2",), T.nq[:], ("nq",), A.mult)
        op("V", lambda e: e.tensor_tensor_scan(T.pc[:], T.ones[:, 0:64], T.wt[:], 0.0, A.mult, A.add), [("ones",), ("wt",)], [("pc",)])
        mm(T.b3[:, 0:64], "b3", T.bo[:], ("bo",), T.pc[:], ("pc",), True, True)
        mm(T.b2[:, 64:128], "b2", T.bo[:], ("bo",), T.pc[:], ("pc",), True, False)
        mm(T.b2[:, 64:128], "b2", T.lm[:], ("lm",), T.wt[:], ("wt",), False, True)
        cpy(T.rt[:, 0:64], ("rt", 0, 64), T.b2[:, 64:128], ("b2",))
        for n in range(8):
            act(T.junk[:, 64 * n:64 * n + 64], ("junk", 64 * n, 64 * n + 64), T.b3[:, 0:64], ("b3",), AF.Sign, bias=T.kch[:, n:n + 1], scale=-1.0, extra=[("kch",)], accum=T.ck[:, n:n + 1], ao=("ck", n, n + 1))
        ts(T.ckl[:], ("ckl",), T.ck[:], ("ck",), 0.5, 32.0, A.mult, A.add)
        src = T.rt[:, 0:72].indirect(T.ckl[:])
        op("V", lambda e: e.tensor_tensor(T.le[:], src, T.kio[:], A.is_le), [("rt",), ("ckl",), ("kio",)], [("le",)])
        ts(T.ckb[:], ("ckb",), T.ck[:], ("ck",), 0.5, 32.0, A.mult, A.add)
        slot_list("b2", "le", False)
        mm(T.b2[:, 0:8], "b2", *I16, T.ckb[:], ("ckb",), False, True)
        cpy(T.jk[:], ("jk",), T.b2[:, 0:8], ("b2",))
        gather("V", T.sab[:, 0:128], ("sab", 0, 128), T.ra, "ra", 0, K + 16, T.jk[:], ("jk",))
        gather("S", T.sab[:, 128:256], ("sab", 128, 256), T.rb, "rb", 0, K + 16, T.jk[:], ("jk",))
        mm(T.b3[:, 0:256], "b3", T.plw[:], ("plw",), T.sab[:], ("sab",), True, True)
        diag("b6", 0, 16, "dp", "sab", 0, 256)
        cpy(T.plr[:], ("plr",), T.b3[:, 0:256], ("b3",))
        cpy(T.plt[:], ("plt",), T.b6[:, 0:16], ("b6",))
        for n in range(16):
            a = 256 * (n % NEQ)
            ts(T.eq[:, a:a + 256], ("eq", a, a + 256), T.plr[:], ("plr",), T.plt[:, n:n + 1], None, A.is_equal, extra=[("plt",)])
            for s in range(2):
                mm(T.b7[:, 0:128], "b7", T.bo[:], ("bo",), T.eq[:, a + 128 * s:a + 128 * s + 128], ("eq", a, a + 256), n == 0 and s == 0, n == 15 and s == 1)
        tt("V", T.dab[:], ("dab",), T.sab[:, 128:256], ("sab",), T.sab[:, 0:128], ("sab",), A.subtract)
        tt("V", T.pd[:], ("pd",), T.plt[:], ("plt",), T.dumc[:], ("dumc",), A.subtract)
        ts(T.cb[:], ("cb",), T.b7[:, 0:128], ("b7",), 2.0, 1.0 / 16, A.is_equal, A.mult)
        ts(T.cp[:], ("cp",), T.b7[:, 0:128], ("b7",), 2.0, co[:, 10:11], A.is_equal, A.mult, extra=[("cols", 10, 11)])
        slot_list("b3", "cb", True)
        tt("V", T.dmv[:], ("dmv",), T.dab[:], ("dab",), T.cp[:], ("cp",), A.mult)
        for s in range(2):
            tt("V", T.of[:, 8 * s:8 * s + 8], ("of", 8 * s, 8 * s + 8), T.b3[:, 0:8], ("b3",), T.pd[:, 8 * s:8 * s + 8], ("pd",), A.mult)
        tt("V", T.nv[:, 0:128], ("nv", 0, 128), T.sab[:, 0:128], ("sab",), T.dmv[:], ("dmv",), A.add)
        tt("V", T.of[:, 16:32], ("of", 16, 32), T.of[:, 0:16], ("of", 0, 16), T.dumc[:], ("dumc",), A.add)
        tt("V", T.nv[:, 128:256], ("nv", 128, 256), T.sab[:, 128:256], ("sab",), T.dmv[:], ("dmv",), A.subtract)
        cpy(T.ofl[:], ("ofl",), T.of[:, 16:32], ("of", 16, 32))
        out = T.pw[:, 0:3 * W + 2 * CAP].indirect(T.ofl[:])
        op("V", lambda e: e.tensor_copy(out, T.nv[:]), [("nv",), ("ofl",)], [("pw",)], None, 1.0)
        if not last:
            for i in range(NT):
                for k in range(2):
                    dma("Y", T.inf[2 * i + k::16, :], ("inf", 0, W, 2 * i + k), T.pw[k::16, W * i:W * i + W], ("pw", W * i, W * i + W, k), "d_rb")
            return
        dma("Y", T.yh[:], ("yh",), T.pw[0::16, 0:3 * W], ("pw", 0, 3 * W, 0), "d_y1")
        dma("Y", T.yl[:], ("yl",), T.pw[1::16, 0:3 * W], ("pw", 0, 3 * W, 1), "d_y1")
        parts = [(384 * i, 384 * i + 384, ("b3", "b6", "b7")[i]) for i in range(NT)]
        for a, b, bank in parts:
            mm(T[bank][:, 0:384], bank, T.idb[:], ("idb",), T.yh[:, a:b], ("yh",), True, False)
            mm(T[bank][:, 0:384], bank, T.idb[:], ("idb",), T.yl[:, a:b], ("yl",), False, True)
        for n, (a, b, bank) in enumerate(parts):
            if n == 1:
                act(T.yf[:, a:b], ("yf", a, b), T[bank][:, 0:384], (bank,), AF.Copy)
            else:
                cpy(T.yf[:, a:b], ("yf", a, b), T[bank][:, 0:384], (bank,))
        dma("Y", T.yn[:], None, T.yf[:], ("yf",), "d_yn1")

    def cursors(last):
        for be in range(2):
            for h in range(4):
                act(T.ltc[:, 24 * be:24 * be + 24, h, :], ("ltc", 384 * be, 384 * be + 384, h), T["st%d" % be][:, 96:192], ("st%d" % be,), AF.Copy, scale=co[:, h:h + 1], extra=[("cols", h, h + 1)])
        for be in range(2):
            for i in range(NT):
                n = 3 * be + i
                mm(T.b5[:, 64 * i + 32 * be:64 * i + 32 * be + 32], "b5", T.ltc[:, 8 * n:8 * n + 8, :, :], ("ltc", 384 * be, 384 * be + 384), T.sel[:], ("sel",), True, True)
        cpy(T.ci[:, 0:192], ("ci", 0, 192), T.b5[:, 0:192], ("b5",))
        ts(T.ci[:, 192:384], ("ci", 192, 384), T.ci[:, 0:192], ("ci", 0, 192), STAMP - 1, None, A.bitwise_and)
        if last:
            cpy(T.ycf[:], ("ycf",), T.ci[:, 192:384], ("ci", 192, 384))
            dma("Y", T.yc[:], None, T.ycf[:], ("ycf",), "d_yc")
        else:
            for i in range(NT):
                a, b = 64 * i, 64 * i + 64
                ts(T.lst[:, a:b], ("lst", a, b), T.ci[:, 192 + a:192 + b], ("ci", 192, 384), W * i, None, A.add)

    def pull(t, last):
        diag("b4", 64, 128, "df", "ra", 0, K)
        cpy(T.kl[:], ("kl",), T.b4[:, 64:128], ("b4",))
        xn = "x%d" % (t + 1)
        for be in range(2):
            a, b = H * be, H * be + H
            ysrc = T[xn][:, 0:W].indirect(T.kl[:, 32 * be:32 * be + 32])
            op("V", lambda e, ysrc=ysrc, a=a, b=b: e.tensor_tensor(T.dd[:, a:b], ysrc, T.wf[:, a:b], A.subtract), [(xn,), ("kl",), ("wf", a, b)], [("dd", a, b)], None, us(1.5 * H))
            D, dn = T["b%d" % be], "b%d" % be
            ts(D[:], (dn,), T.dd[:, a:b], ("dd", a, b), 8.0, -8.0, A.min, A.max)
            tt("V", T.wf[:, a:b], ("wf", a, b), D[:], (dn,), T.wf[:, a:b], ("wf", a, b), A.add)
            if last:
                dma("S", T.yw[:, a:b], None, T.wf[:, a:b], ("wf", a, b), "d_yw%d" % be)

    types_in()
    for t in range(ROUNDS):
        last = t == ROUNDS - 1
        streams = [(record(finds, 0, t), 0.0), (record(finds, 1, t), FB)]
        if t == 0:
            streams.append((record(later), LB))
        merge(*streams)
        merge((record(swap, last), 0.0), (record(cursors, last), CB), (record(pull, t, last), PB))
    for s in sorted(total):
        know("G", s, total[s])
